import numpy as np, ml_dtypes
CORES = [16,17,18,19,32,33,34,35]
N = 8
BF = ml_dtypes.bfloat16
def gentries(a):
    return np.ascontiguousarray(a.reshape(8, 16, -1).transpose(0, 2, 1)).reshape(8, -1)
def gtable(e):
    e = np.asarray(e); return np.ascontiguousarray(e.reshape(8, -1, 16).transpose(0, 2, 1)).reshape(128, -1).astype(np.int32)
W, R, NR, TV = 4096, 8, 512, 3
K = R * NR; NONE = W - 1; SH = (N, 8, R, NR)
def hsh(a, b):
    return (((a * b) >> 5) + 37 * a + b) & (W - 1)
def pack(x, y, g, a, b, t):
    o = {"xt": np.ascontiguousarray(x.reshape(N, 128, W)).astype(np.float32).astype(BF), "yv": np.ascontiguousarray(y.reshape(N, 128, TV * NR)).astype(np.float32).astype(BF)}
    for k, v in (("gl", g), ("al", a), ("bl", b), ("th", t)): o[k] = np.stack([gtable(w.reshape(8, -1)) for w in v])
    return o
def robots(rng, share, mem):
    g = np.where(rng.random(SH) < share, rng.integers(0, NONE, SH), NONE); keep = rng.random(SH) < mem
    return g, np.where(keep, rng.integers(0, NONE, SH), NONE), np.where(keep, rng.integers(0, NONE, SH), NONE)
def pool(rng, goals, m):
    a = rng.permutation(NONE)[:64]; a[0] = 64; a[1] = 128
    lut = np.zeros(W, bool); lut[goals] = True
    i, j = np.nonzero(lut[hsh(a[:, None], np.arange(NONE)[None, :])]); s = rng.integers(0, len(i), m)
    return a[i[s]], j[s]
def halves(rng, x, y, q, e):
    near = np.zeros(W, bool); near[rng.permutation(NONE)[:W // 2]] = True
    x[q, e] = np.where(near[None, :], rng.integers(0, 64, (16, W)), rng.integers(128, 256, (16, W)))
    y[q, e, :, 0] = rng.integers(0, 64, (16, NR))
    return near
def pairs(rng, near):
    far = rng.permutation(np.nonzero(~near[:NONE])[0]); a = far[:128]
    i, j = np.nonzero(near[hsh(a[:, None], far[None, :])]); s = rng.permutation(len(i))
    u, v = a[i[s]], far[j[s]]
    return u, v, hsh(u, v)
def setup_inputs(rng):
    x = rng.integers(0, 256, (N, 8, 16, W)); y = rng.integers(0, 256, (N, 8, 16, TV, NR))
    g, a, b = robots(rng, rng.choice(np.array([0.3, 0.6, 0.9, 1.0]), (N, 8, 1, NR)), 0.4)
    return pack(x, y, g, a, b, rng.integers(900, 1700, SH))
def setup_inputs_clash(rng):
    x = rng.integers(0, 256, (N, 8, 16, W)); y = rng.integers(0, 256, (N, 8, 16, TV, NR)); g, a, b = robots(rng, 1.0, 0.3)
    for q in range(N):
        for e in range(8):
            goals = np.concatenate([np.array([0, W - 2]), rng.integers(1, W - 2, 2)]); c = rng.integers(0, 256, 16)
            x[q, e][:, goals] = c[:, None]; y[q, e][:, 0, :] = c[:, None]
            u, v = pool(rng, goals, (R // 2) * NR)
            g[q, e, 0::2] = u.reshape(R // 2, NR); g[q, e, 1::2] = v.reshape(R // 2, NR)
    g = np.where((rng.random((N, 8, 1, NR)) < 0.3) | (rng.random(SH) < 0.1), NONE, g)
    for q in range(N):
        for s, e in enumerate(rng.permutation(8)[:2]):
            u, v, n = pairs(rng, halves(rng, x, y, q, e))
            if s == 0:
                w = np.nonzero(n == n[0])[0]; i = w[rng.integers(0, len(w), K // 2)]
            else:
                i = rng.integers(0, len(n), K // 2); i[:NR] = rng.permutation(np.unique(n, return_index=True)[1])[:NR]
            g[q, e, 0::2] = u[i].reshape(R // 2, NR); g[q, e, 1::2] = v[i].reshape(R // 2, NR)
    return pack(x, y, g, a, b, rng.integers(900, 1700, SH))
def setup_inputs_ties(rng):
    s = rng.integers(0, 2, (N, 8, 1, 1)) * 3 + 1
    x = 100 + s * rng.integers(0, 8, (N, 8, 16, W)); y = 100 + s[..., None] * rng.integers(0, 8, (N, 8, 16, TV, NR))
    g, a, b = robots(rng, rng.choice(np.array([0.4, 0.7, 1.0]), (N, 8, 1, NR)), 0.6)
    return pack(x, y, g, a, b, np.where(s == 1, rng.integers(0, 60, SH), rng.integers(60, 200, SH)))
def setup_inputs_corners(rng):
    x = rng.integers(0, 256, (N, 8, 16, W)); y = rng.integers(0, 256, (N, 8, 16, TV, NR)); g, a, b = robots(rng, 1.0, 1.0)
    kd = rng.integers(0, 11, (N, 8, 1, NR)); k = np.arange(R)[None, None, :, None]
    none = g.copy()
    for q in range(N):
        for e in range(8):
            u, v = pool(rng, np.array([NONE]), (R // 2) * NR)
            none[q, e, 0::2] = u.reshape(R // 2, NR); none[q, e, 1::2] = v.reshape(R // 2, NR)
    g = np.where(kd == 6, g[:, :, :1], np.where(kd == 8, none, np.where((kd == 10) & (k % 2 == 0), 0, g)))
    full = (kd == 1) | ((kd == 2) & (k % 2 == 0)) | ((kd == 3) & (k % 2 == 1)) | ((kd == 4) & (k == R - 1)) | ((kd == 5) & (k == 0)) | (kd == 6) | ((kd == 7) & (k % 4 < 2)) | (kd == 8) | ((kd == 9) & (rng.random(SH) < 0.5)) | (kd == 10)
    g = np.where(full, g, NONE)
    a = np.where((kd == 9) | ((kd == 10) & (rng.random(SH) < 0.5)), NONE, a); b = np.where(kd == 7, NONE, b)
    a = np.where(rng.random(SH) < 0.05, rng.choice(np.array([0, W - 2]), SH), a)
    t = rng.choice(np.array([0, 4080, 1300, 1400]), SH, p=[0.3, 0.2, 0.25, 0.25])
    for q in range(N):
        for s, e in enumerate(rng.permutation(8)[:2]):
            near = halves(rng, x, y, q, e); far = np.nonzero(~near[:NONE])[0]
            second = (np.arange(R)[:, None] + rng.integers(0, 2, NR)[None, :]) % 2 == 0
            if s == 0:
                a[q, e] = rng.integers(0, NONE, (R, NR)); t[q, e] = rng.integers(0, 1000, (R, NR))
            else:
                far = far[near[hsh(NONE, far)]]; w = rng.random((R, NR)) < 0.5
                a[q, e] = np.where(w, NONE, a[q, e]); t[q, e] = np.where(w, t[q, e], 4080)
            g[q, e] = np.where(second, far[rng.integers(0, len(far), (R, NR))], NONE)
    return pack(x, y, g, a, b, t)
def setup_inputs_ends(rng):
    v = 255 * rng.integers(0, 2, (N, 1, 1, 1)); e = rng.integers(0, 4, (N, 8, 1, W))
    x = np.where(e == 0, 0, np.where(e == 1, 255, 255 * rng.integers(0, 2, (N, 8, 16, W))))
    near = (rng.random((N, 8, 1, W)) < 0.25) & (np.arange(16)[None, None, :, None] == rng.integers(0, 16, (N, 8, 1, W)))
    x = np.where(near, np.abs(x - 1), x)
    x[..., 0] = v[..., 0]; x[..., W - 2] = v[..., 0]; x[..., W - 74] = 255 - v[..., 0]
    e = rng.integers(0, 3, (N, 8, 1, TV, NR)); y = np.where(e == 0, 0, np.where(e == 1, 255, 255 * rng.integers(0, 2, (N, 8, 16, TV, NR))))
    S = np.array([0, 1, int(rng.integers(2, NR - 2)), NR - 2, NR - 1])
    k = np.arange(R)[None, None, :, None]
    ty = rng.choice(np.array([0, 1, 2]), (N, 8, 1, NR), p=[0.6, 0.3, 0.1])
    ty[..., S] = 1
    g = np.where(ty == 0, rng.choice(np.array([0, NONE]), SH), np.where(ty == 1, np.where(k % 2 == 0, W - 2, 0), np.where(rng.random(SH) < 0.3, NONE, rng.integers(0, NONE, SH))))
    a = rng.choice(np.array([0, NONE, W - 2]), SH, p=[0.45, 0.45, 0.1]); b = rng.choice(np.array([0, NONE, W - 2]), SH, p=[0.45, 0.45, 0.1])
    t = rng.choice(np.array([0, 4080, 4079, 1]), SH, p=[0.4, 0.4, 0.1, 0.1])
    far = np.roll(v, -1, axis=0)
    for i in S:
        y[:, :, :, 0, i] = 255 - v[..., 0]; y[:, :, :, 1, i] = 255 - far[..., 0]
        t[:, :, :, i] = 4080 - 4 * R - (np.arange(R)[None, None, :] // 2) % 2
    return pack(x, y, g, a, b, t)
def setup_inputs_spread(rng):
    x = np.minimum((np.exp2(8 * rng.random((N, 8, 1, W))) * rng.random((N, 8, 16, W))).astype(np.int64), 255)
    y = np.minimum((np.exp2(8 * rng.random((N, 8, 1, TV, NR))) * rng.random((N, 8, 16, TV, NR))).astype(np.int64), 255)
    g, a, b = robots(rng, rng.random((N, 8, 1, NR)), rng.random((N, 8, 1, NR)))
    few = rng.random((N, 8, 1, NR)) < 0.5
    g = np.where(few & (g != NONE), np.minimum((NONE * rng.random(SH) ** 6).astype(np.int64), NONE - 1), g)
    t = np.minimum(np.exp2(12 * rng.random(SH)).astype(np.int64) - 1, 4080)
    return pack(x, y, g, a, b, t)
def check_inputs(d):
    bad = []
    for k, hi in (("xt", 255), ("yv", 255), ("gl", NONE), ("al", NONE), ("bl", NONE), ("th", 4080)):
        v = np.asarray(d[k]).astype(np.float64)
        if not (np.all(v >= 0) and np.all(v <= hi)): bad.append("range of " + k)
        elif np.any(v != np.floor(v)): bad.append("whole numbers of " + k)
    return bad
def reference(xt, yv, gl, al, bl, th):
    x = xt.astype(np.float32).astype(np.int32).reshape(N, 8, 16, W); y = yv.astype(np.float32).astype(np.int32).reshape(N, 8, 16, TV, NR)
    g, a, b, h = [np.stack([gentries(v) for v in w]).astype(np.int32).reshape(N, 8, R, NR) for w in (gl, al, bl, th)]
    c = np.zeros((N, NR), np.int32); row = np.arange(R)[None, :, None]; rob = np.arange(NR)[None, :]
    for t in range(TV):
        for r in range(N):
            q = (r + t) % N; G, A, B = g[r].copy(), a[r].copy(), b[r].copy()
            G1 = np.roll(G, -1, axis=1); n = hsh(G, G1); view = y[r][:, :, t][:, :, None, :]
            xg = np.take_along_axis(x[q], G.reshape(8, 1, K), 2); xn = np.take_along_axis(x[q], n.reshape(8, 1, K), 2)
            dg = np.add.reduce(np.abs(xg.reshape(8, 16, R, NR) - view), axis=1); dn = np.add.reduce(np.abs(xn.reshape(8, 16, R, NR) - view), axis=1)
            dg1 = np.roll(dg, -1, axis=1); full = G != NONE; full1 = np.roll(full, -1, axis=1)
            opens = full & (A != NONE) & ~full1 & (dg > h[r] + c[r][None, None, :])
            opened = np.roll(opens, 1, axis=1)
            merge = full & full1 & ~np.roll(opens, -1, axis=1) & ((row + t) % 2 == 0) & (n != NONE) & (dn < np.minimum(dg, dg1))
            gone = np.roll(merge, 1, axis=1)
            take = ~full & ~opened & full1 & (n != NONE) & (dn < dg1)
            some = np.any(merge, axis=1); low = np.argmax(merge, axis=1)
            i0 = low * NR + rob; i1 = ((low + 1) % R) * NR + rob
            val = (np.take_along_axis(xg, i0[:, None, :], 2) + np.take_along_axis(xg, i1[:, None, :], 2)) >> 1
            goal = np.take_along_axis(n.reshape(8, K), i0, 1)
            for e in range(8):
                w = np.nonzero(some[e])[0]; u, first = np.unique(goal[e][w], return_index=True)
                x[q, e][:, u] = val[e][:, w[first]]
            clear = opens | opened | gone | take
            g[r] = np.where(opens, A, np.where(opened, np.roll(B, 1, axis=1), np.where(merge | take, n, np.where(gone, NONE, G))))
            na = np.where(merge, G, np.where(clear, NONE, A)); nb = np.where(merge, G1, np.where(clear, NONE, B))
            a[r] = na; b[r] = nb; c[r] = np.add.reduce(merge.astype(np.int32), axis=(0, 1))
    o = [np.stack([gtable(v.reshape(8, -1)) for v in w]).astype(np.float32) for w in (g, a, b)]
    return {"og": o[0], "oa": o[1], "ob": o[2], "ox": x.reshape(N, 128, W).astype(np.float32).astype(BF)}

@@ -1,0 +1,426 @@
+import numpy as np
+from concourse.mybir import AluOpType as A, ActivationFunctionType as F
+
+M = 4
+NB = 32 // M
+NE = NB * M * (M - 1) // 2
+f32, bf, i32, u16 = "float32", "bfloat16", "int32", "uint16"
+SCRATCH = {
+    "win": ("sbuf", [128, 4608], bf), "sv": ("sbuf", [128, 16], bf),
+    "yv0": ("sbuf", [128, 1024], bf), "yv1": ("sbuf", [128, 1024], bf), "yv2": ("sbuf", [128, 1024], bf),
+    "yi1": ("sbuf", [128, 1024], bf), "yi2": ("sbuf", [128, 1024], bf),
+    "gn": ("sbuf", [128, 4, 2, 32], i32), "an": ("sbuf", [128, 4, 2, 32], i32), "bn": ("sbuf", [128, 4, 2, 32], i32),
+    "tn": ("sbuf", [128, 4, 2, 32], i32), "tf0": ("sbuf", [128, 8, 32], f32),
+    "ti1": ("sbuf", [128, 8, 32], f32), "ti2": ("sbuf", [128, 8, 32], f32),
+    "l0": ("sbuf", [128, 384], u16), "l1": ("sbuf", [128, 384], u16), "l2": ("sbuf", [128, 384], u16),
+    "lo1": ("sbuf", [128, 384], u16), "lo2": ("sbuf", [128, 384], u16),
+    "dd": ("sbuf", [128, 6144], bf), "ab": ("sbuf", [128, 6144], bf),
+    "E": ("sbuf", [128, 8, 32], bf), "AE": ("sbuf", [128, 8, 32], bf), "O": ("sbuf", [128, 8, 32], bf),
+    "UX": ("sbuf", [128, 8, 32], bf), "Mf": ("sbuf", [128, 4, 32], bf), "Uf": ("sbuf", [128, 8, 32], bf),
+    "Eo": ("sbuf", [128, 4, 32], bf), "Cb": ("sbuf", [128, 1, 32], bf),
+    "thr": ("sbuf", [128, 8, 32], f32), "dsb": ("sbuf", [128, 8, 32], f32), "mn": ("sbuf", [128, 4, 32], f32),
+    "vk": ("sbuf", [128, 4, 3, 32], f32), "keys": ("sbuf", [128, 4, 3, 32], f32), "t1": ("sbuf", [128, 2, 3, 32], f32),
+    "t2": ("sbuf", [128, 3, 32], f32), "fall": ("sbuf", [128, 3, 32], f32), "t3": ("sbuf", [128, 3, 32], i32),
+    "tv": ("sbuf", [128, 3, 32], i32), "lgg": ("sbuf", [128, 64], u16), "hi": ("sbuf", [128, 32], bf),
+    "lw": ("sbuf", [128, 32], bf), "own": ("sbuf", [128, 16, NB, M], f32), "eq": ("sbuf", [128, 16, 32], bf), "ee": ("sbuf", [128, 16, NE], bf), "ce": ("sbuf", [128, NE], bf),
+    "gab": ("sbuf", [128, 1024], bf), "vf": ("sbuf", [128, 512], f32), "vals": ("sbuf", [128, 512], bf), "dm": ("sbuf", [128, 32], i32),
+    "dst": ("sbuf", [128, 32], u16),
+    "oab": ("sbuf", [128, 16, 32], f32), "kab": ("sbuf", [128, 16, 32], f32), "mz": ("sbuf", [128, 8, 32], f32),
+    "uz": ("sbuf", [128, 4, 32], f32), "vz": ("sbuf", [128, 8, 32], f32), "X": ("sbuf", [128, 8, 32], f32),
+    "P": ("sbuf", [128, 8, 32], i32), "H": ("sbuf", [128, 8, 32], i32), "NQ": ("sbuf", [128, 8, 32], i32),
+    "IDX": ("sbuf", [128, 8, 32], i32),
+    "fog": ("sbuf", [128, 4, 2, 32], f32), "foab": ("sbuf", [128, 2, 4, 2, 32], f32),
+    "fig": ("sbuf", [128, 4, 2, 32], f32), "fiab": ("sbuf", [128, 2, 4, 2, 32], f32),
+    "ones": ("sbuf", [128, 256], bf), "SS": ("sbuf", [128, 2048], bf), "BB": ("sbuf", [128, 16, 128], bf),
+    "MK": ("sbuf", [128, 16, 128], bf), "SG": ("sbuf", [128, 128], bf),
+    "pi": ("sbuf", [128, 1], i32), "pa": ("sbuf", [128, 1], i32), "pb": ("sbuf", [128, 1], i32),
+    "pm": ("sbuf", [128, 1], f32), "pg": ("sbuf", [128, 1], f32), "io8": ("sbuf", [128, 8], f32),
+    "iop": ("sbuf", [128, 8, 16], f32), "bm8": ("sbuf", [128, 8], f32), "ioi": ("sbuf", [128, 32], f32),
+}
+for _n in ("st0", "st1", "st2", "po1", "po2"):
+    SCRATCH[_n] = ("sbuf", [128, 33, 32], f32)
+WB = {"I1": 1, "Im1": -1, "I2": 2, "Im2": -2, "I8k": 8192, "I16k": 16384, "Im16k": -16384, "I1920": 1920, "I28": 28}
+WF = {"J1": 1, "Jm1": -1, "Jm101": -101, "Jm129": -129}
+CM = {"c230": -230 / 128, "cm1": -1 / 128, "cm2048": -16, "cp1": 1 / 128, "cmh": -0.5 / 128}
+for _n in WB: SCRATCH[_n] = ("sbuf", [128, 128], bf)
+for _n in WF: SCRATCH[_n] = ("sbuf", [128, 128], f32)
+for _n in CM: SCRATCH[_n] = ("sbuf", [128, 128], bf)
+for _n in ("b0", "b3", "b4", "b5", "b6", "b7"): SCRATCH[_n] = ("psum", [128, 16, 32], f32)
+for _n in ("b1", "b2"): SCRATCH[_n] = ("psum", [128, 16, NB, M], f32)
+NDMA = 16
+ARR = ["yi1", "yi2", "ti1", "ti2", "l1", "l2", "s1a", "s1b", "s2a", "s2b", "fg", "fab"]
+SEMAPHORES = ["qv", "qs", "qt", "qg", "loc"] + ["d%d" % k for k in range(NDMA)] + ["a_" + n for n in ARR]
+_cache = {}
+
+
+def rank_program(g, core, T, topo):
+    rank = T.rank_of(core)
+    if rank is None:
+        return
+    N = len(T.cores)
+    eng = {"v": g.vector, "s": g.scalar, "t": g.tensor, "g": g, "y": g.sync}
+    cnt = {}
+    known = {q: {} for q in eng}
+    hist = {n: [] for n in SCRATCH}
+
+    def X(name, *idx):
+        key = (name,) + tuple(("s", i.start, i.stop, i.step) if isinstance(i, slice) else i for i in idx)
+        if key not in _cache:
+            shp = SCRATCH[name][1][1:]
+            a = np.arange(int(np.prod(shp))).reshape(shp)[idx].ravel()
+            b = np.zeros(int(np.prod(shp)), np.uint8)
+            b[a] = 1
+            _cache[key] = int.from_bytes(np.packbits(b).tobytes(), "big")
+        return (T[name][(slice(None),) + idx], name, _cache[key])
+
+    def sync(q, rd, wr):
+        need = {}
+        for regs, w in ((rd, False), (wr, True)):
+            for r in regs:
+                psum = SCRATCH[r[1]][0] == "psum"
+                for (m, pw, pq, sem, c, clk) in hist[r[1]]:
+                    if psum and pq != q:
+                        hit = True
+                    elif psum and q == "t":
+                        hit = False
+                    else:
+                        hit = bool(m & r[2]) and (pw or w)
+                    if hit and known[q].get(sem, 0) < c and (sem not in need or need[sem][0] < c):
+                        need[sem] = (c, clk)
+        for sem in sorted(need, key=lambda s: -len(need[s][1])):
+            c, clk = need[sem]
+            if known[q].get(sem, 0) >= c: continue
+            eng[q].wait_ge(T.sem[sem], c)
+            for k in clk: known[q][k] = max(known[q].get(k, 0), clk[k])
+
+    def record(q, rd, wr, sem, c):
+        clk = dict(known[q]); clk[sem] = c
+        for regs, w in ((rd, False), (wr, True)):
+            for r in regs:
+                h = hist[r[1]]
+                if w:
+                    h[:] = [e for e in h if (e[0] & ~r[2]) or clk.get(e[3], 0) < e[4]]
+                else:
+                    h[:] = [e for e in h if e[1] or e[2] != q or (e[0] & ~r[2])]
+                h.append((r[2], w, q, sem, c, clk))
+
+    def emit(q, call, rd, wr):
+        sem = "q" + q
+        sync(q, rd, wr)
+        cnt[sem] = cnt.get(sem, 0) + 1
+        call().then_inc(T.sem[sem], 1)
+        record(q, rd, wr, sem, cnt[sem])
+
+    v, s, te = g.vector, g.scalar, g.tensor
+    def tt(o, a, b, op): emit("v", lambda: v.tensor_tensor(o[0], a[0], b[0], op), [a, b], [o])
+    def ts(o, a, s1, s2, op0, op1=None):
+        sc = [x for x in (s1,) if isinstance(x, tuple)]
+        p1 = s1[0] if sc else s1
+        if op1 is None: emit("v", lambda: v.tensor_scalar(o[0], a[0], p1, None, op0), [a] + sc, [o])
+        else: emit("v", lambda: v.tensor_scalar(o[0], a[0], p1, s2, op0, op1), [a] + sc, [o])
+    def cp(o, a): emit("v", lambda: v.tensor_copy(o[0], a[0]), [a], [o])
+    def ms(o, c): emit("v", lambda: v.memset(o[0], c), [], [o])
+    def act(o, a, f=F.Identity, bias=0.0, scale=1.0):
+        if isinstance(scale, tuple): emit("s", lambda: s.activation(o[0], a[0], f, scale=scale[0]), [a, scale], [o])
+        elif bias == 0.0: emit("s", lambda: s.activation(o[0], a[0], f, scale=scale), [a], [o])
+        else: emit("s", lambda: s.activation(o[0], a[0], f, bias=bias, scale=scale), [a], [o])
+    def mm(o, w, r, first, last): emit("t", lambda: te.matmul(o[0], w[0], r[0], first, last), [w, r], [o])
+    W = lambda n: X(n)
+    ndma = [0]
+    def dma(q, o, a, rd, wr):
+        sem = "d%d" % ndma[0]; ndma[0] += 1
+        sync(q, rd, wr)
+        eng[q].dma_start(o, a).then_inc(T.sem[sem], 16)
+        cnt[sem] = 16
+        record(q, rd, wr, sem, 16)
+    def nengines(a, b): return len(topo.engines(a, b))
+    def send(to, o, i, sem):
+        dst = T.cores[to % N]
+        sync("g", [i], [])
+        rid, pid, _ = topo.addr(dst)
+        cnt["loc"] = cnt.get("loc", 0) + nengines(core, dst)
+        g.remote_dma(o[0], i[0], T.sem["a_" + sem], T.sem.loc, pid, rid, topo.mask(core, dst))
+    def arrives(frm, sem, o):
+        c = nengines(T.cores[frm % N], core)
+        cnt["a_" + sem] = c
+        hist[o[1]].append((o[2], True, "r", "a_" + sem, c, {"a_" + sem: c}))
+    S = slice
+    def rows(n, a, b): return X(n, S(a, b))
+
+    dma("y", T.gn[:], T.gl[:], [], [W("gn")])
+    dma("y", T.win[:, 0:4096], T.xt[:], [], [X("win", S(0, 4096))])
+    for k in (0, 1, 2):
+        if k == 1:
+            for n, src in (("an", T.al), ("bn", T.bl), ("tn", T.th)): dma("y", T[n][:], src[:], [], [W(n)])
+        for h in (0, 1):
+            n = "yv%d" % k
+            dma("y", T[n][:, h * 512:h * 512 + 512], T.yv[:, k * 512:k * 512 + 512], [], [X(n, S(h * 512, h * 512 + 512))])
+    for n, k in (("yi1", 1), ("ti1", 1), ("yi2", 2), ("ti2", 2)): arrives(rank - k, n, W(n))
+    for k in (1, 2):
+        arrives(rank - 1, "l%d" % k, W("l%d" % k))
+        arrives(rank - 1, "s%da" % k, rows("st%d" % k, 0, 16))
+        arrives(rank - 1, "s%db" % k, rows("st%d" % k, 16, 33))
+    arrives(rank + 2, "fg", W("fig")); arrives(rank + 2, "fab", W("fiab"))
+
+    emit("g", lambda: g.iota(T.pi[:], [[0, 1]], 0, 1), [], [W("pi")])
+    ms(W("ones"), 1.0)
+    big = dict(allow_small_or_imprecise_dtypes=True)
+    emit("g", lambda: g.affine_select(T.I1[:], T.ones[:, 0:128], [[-1, 128]], A.is_equal, 0.0, 0, 1), [X("ones", S(0, 128))], [W("I1")])
+    emit("g", lambda: g.iota(T.io8[:], [[1, 8]], 0, 0, **big), [], [W("io8")])
+    emit("g", lambda: g.iota(T.iop[:], [[0, 8], [1, 16]], 0, 0, **big), [], [W("iop")])
+    emit("g", lambda: g.iota(T.ioi[:], [[16, 32]], 4096, 0, **big), [], [W("ioi")])
+    ms(W("SS"), 0.0)
+    for n in CM: ms(W(n), CM[n])
+    ts(W("pa"), W("pi"), 15, None, A.bitwise_and)
+    ts(W("pb"), W("pi"), 4, None, A.arith_shift_right)
+    cp(W("pm"), W("pa")); cp(W("pg"), W("pb"))
+    ts(W("bm8"), W("io8"), W("pg"), None, A.is_equal)
+    ts(W("SG"), W("iop"), W("pm"), None, A.is_equal)
+    ms(X("fall", S(1, 3)), 0.0)
+    ts(X("fall", 0), W("ioi"), W("pm"), None, A.add)
+    for n in ("J1", "Jm1", "Jm101", "Jm129"): act(W(n), W("I1"), F.Identity, scale=float(WF[n]))
+    for n in ("I1920", "I28"): act(W(n), W("I1"), F.Identity, scale=float(WB[n]))
+    for e in range(8):
+        act(X("SS", S(16 * e, 16 * e + 129 * 15 + 1, 129)), X("ones", S(0, 16)), F.Identity, scale=X("bm8", S(e, e + 1)))
+    for n in ("Im1", "I2", "Im2", "I8k", "I16k", "Im16k"): act(W(n), W("I1"), F.Identity, scale=float(WB[n]))
+
+    def pieces(sh): return {0: [(0, 4, 0)], 1: [(0, 3, 1), (3, 4, 0)], -1: [(1, 4, 0), (0, 1, 3)]}[sh]
+    def add(bank, base, w, src, sbase, sh, first=False, last=False):
+        ps = pieces(sh)
+        for j, (a, b, c) in enumerate(ps):
+            mm(rows(bank, base + a, base + b), W(w), rows(src, sbase + c, sbase + c + b - a), first and j == 0, last and j == len(ps) - 1)
+
+    def index_stage(po, lo, meanwhile=None):
+        ts(rows("X", 4, 8), rows("b7", 0, 4), -2047.0, -4127.0, A.is_equal, A.mult)
+        act(rows(po, 4, 8), rows("b7", 0, 4), F.Identity, bias=2047.0)
+        act(W("Eo"), rows("b7", 0, 4), F.Relu, bias=-2046.0, scale=-1.0)
+        ts(X(lo, S(0, 128)), rows("b6", 0, 4), -1.0, 2048.0, A.mult, A.add)
+        ts(rows("X", 0, 4), rows("b6", 0, 4), 2048.0, None, A.add)
+        tt(rows("P", 4, 7), rows("X", 4, 7), rows("b6", 1, 4), A.mult)
+        tt(rows("P", 7, 8), rows("X", 7, 8), rows("b6", 0, 1), A.mult)
+        act(rows(po, 8, 12), rows("b6", 0, 4), F.Identity, bias=2047.0)
+        tt(rows("P", 0, 4), rows("X", 0, 4), rows("b7", 0, 4), A.mult)
+        one = X("ones", S(0, 128))
+        mm(rows("b5", 4, 8), W("cm1"), one, True, False)
+        add("b5", 4, "Jm1", po, 4, 0)
+        add("b5", 4, "I1920", "Eo", 0, 0)
+        add("b5", 4, "I28", "Eo", 0, 0, last=True)
+        mm(rows("b5", 0, 4), W("c230"), one, True, False)
+        add("b5", 0, "Jm129", po, 4, 0)
+        add("b5", 0, "Jm101", po, 8, 0, last=True)
+        ts(W("H"), W("P"), 5, None, A.arith_shift_right)
+        if meanwhile: meanwhile()
+        tt(W("NQ"), W("H"), rows("b5", 0, 8), A.add)
+        ts(W("IDX"), W("NQ"), 4095, None, A.bitwise_and)
+        cp(X(lo, S(128, 384)), W("IDX"))
+
+    def index_rest(po):
+        ts(rows(po, 0, 4), rows("IDX", 0, 4), -1.0, 4095.0, A.mult, A.add)
+        ts(rows(po, 12, 16), rows("IDX", 4, 8), -1.0, 4095.0, A.mult, A.add)
+
+    for h in (0, 1): ts(rows("b%d" % (6 + h), 0, 4), X("gn", S(0, 4), h), -1.0, 2048.0, A.mult, A.add)
+    index_stage("st0", "l0")
+    index_rest("st0")
+    ms(W("BB"), 1.0); ms(W("MK"), 8192.0)
+    def home_rest():
+        for n, b in (("an", 16), ("bn", 24)):
+            for h in (0, 1): ts(rows("st0", b + 4 * h, b + 4 * h + 4), X(n, S(0, 4), h), -1.0, 4095.0, A.mult, A.add)
+        for h in (0, 1): cp(rows("tf0", 4 * h, 4 * h + 4), X("tn", S(0, 4), h))
+        for k in (1, 2): send(rank + k, W("ti%d" % k), W("tf0"), "ti%d" % k)
+    for k in (1, 2): send(rank + k, W("yi%d" % k), W("yv%d" % k), "yi%d" % k)
+    emit("g", lambda: g.affine_select(T.BB[:], T.BB[:], [[-1, 16], [-16, 8], [0, 16]], A.is_equal, 0.0, 0, 1), [W("BB")], [W("BB")])
+    emit("g", lambda: g.affine_select(T.MK[:], T.MK[:], [[0, 16], [-16, 8], [-1, 16]], A.is_equal, 0.0, 0, 1), [W("MK")], [W("MK")])
+    emit("g", lambda: g.affine_select(T.MK[:], T.MK[:], [[-1, 16], [0, 8], [1, 16]], A.is_gt, 0.0, 0, 0), [W("MK")], [W("MK")])
+    cp(X("sv", S(0, 1)), X("win", S(4095, 4096)))
+    ms(X("win", S(4095, 4096)), 512.0)
+
+    CALLS = [(0, 64), (64, 64), (256, 64), (320, 64), (128, 64), (192, 32), (224, 32)]
+    def visit(t):
+        st, ls, yv, th = "st%d" % t, "l%d" % t, ("yi%d" % t if t else "yv0"), ("ti%d" % t if t else "tf0")
+
+        def gather(c, n):
+            e = 16 * n
+            o, off, vw, wn = X("dd", S(16 * c, 16 * c + e)), X(ls, S(c, c + n)), X(yv, S(0, e)), X("win", S(0, 4096))
+            emit("v", lambda: v.tensor_tensor(o[0], T.win[:, 0:4096].indirect(off[0]), vw[0], A.subtract), [wn, off, vw], [o])
+        def size(c, n): act(X("ab", S(16 * c, 16 * c + 16 * n)), X("dd", S(16 * c, 16 * c + 16 * n)), F.Abs)
+        def total(c, n):
+            bank, r0 = ("b1", (c - 128) // 32) if 128 <= c < 256 else ("b0", c // 32 if c < 128 else c // 32 - 4)
+            for j in range(16):
+                mm(rows(bank, r0, r0 + n // 32), X("SS", S(128 * j, 128 * j + 128)), X("ab", S(16 * c + j, 16 * c + 16 * n, 16)),
+                   j == 0 and bank == "b0", j == 15 and (bank == "b0" or c == 192))
+        def prep_a():
+            act(rows("E", 0, 4), rows(st, 8, 12), F.Relu, bias=1.0, scale=-1.0)
+            act(rows("E", 4, 8), rows(st, 4, 8), F.Relu, bias=1.0, scale=-1.0)
+            for a in range(4):
+                act(X("vk", a), X(st, S(a, 12, 4)), F.Identity, bias=float(4095 + 8192 * (4 - a)), scale=-1.0)
+        def prep_b():
+            act(W("AE"), rows(st, 16, 24), F.Relu, bias=1.0, scale=-1.0)
+            if t: act(W("Cb"), rows(st, 32, 33), F.Copy)
+            mm(rows("b6", 0, 8), W("I16k"), rows("E", 0, 8), True, False)
+            mm(rows("b6", 0, 8), W("I16k"), rows("AE", 0, 8), False, False)
+            add("b6", 0, "Im16k", "E", 4, 0)
+            add("b6", 4, "Im16k", "E", 0, 1)
+            if t == 1:
+                add("b6", 0, "J1", th, 4, 0); add("b6", 4, "J1", th, 0, 1)
+            else:
+                mm(rows("b6", 0, 8), W("J1"), rows(th, 0, 8), False, t == 0)
+            if t:
+                for k in range(8): mm(rows("b6", k, k + 1), W("I1"), W("Cb"), False, k == 7)
+
+        for k, (c, n) in enumerate(CALLS):
+            gather(c, n)
+            if k == 1 and t == 0: home_rest()
+        for k, (c, n) in enumerate(CALLS):
+            size(c, n)
+            if k == 1: prep_a()
+            if k == 2: prep_b()
+            if k == 4:
+                mm(rows("b1", 0, 4), W("I8k"), rows("E", 4, 8), True, False)
+                act(W("thr"), rows("b6", 0, 8), F.Identity, bias=16384.0)
+            if k < 5: total(c, n)
+            if k == 6: total(192, 64)
+        tt(W("O"), rows("b0", 0, 8), W("thr"), A.is_gt)
+        act(W("dsb"), rows("b0", 0, 8), F.Copy)
+        tt(W("mn"), rows("b0", 0, 4), rows("dsb", 4, 8), A.min)
+        tt(rows("UX", 4, 7), rows("b0", 4, 7), rows("dsb", 1, 4), A.is_lt)
+        tt(rows("UX", 7, 8), rows("b0", 7, 8), rows("dsb", 0, 1), A.is_lt)
+        mm(rows("b5", 0, 8), W("I1"), W("O"), True, True)
+        mm(rows("b5", 8, 16), W("I1"), W("O"), True, True)
+        mm(rows("b3", 0, 4), W("Im1"), rows("E", 0, 4), True, False)
+        add("b3", 0, "Im1", "O", 4, 0)
+        mm(rows("b2", 0, 8), W("I1"), W("E"), True, False)
+        add("b2", 0, "Im1", "O", 4, 0)
+        add("b2", 0, "Im2", "O", 4, -1)
+        add("b2", 4, "Im1", "O", 0, 0)
+        add("b2", 4, "Im1", "E", 0, 1)
+        add("b2", 4, "I1", "UX", 4, 0)
+        tt(rows("UX", 0, 4), rows("b1", 0, 4), W("mn"), A.is_lt)
+        tt(W("oab"), W("b5"), rows(st, 16, 32), A.mult)
+        add("b3", 0, "I1", "UX", 0, 0, last=True)
+        add("b2", 0, "I2", "UX", 0, 0, last=True)
+        ts(W("Mf"), rows("b3", 0, 4), 0.5, None, A.is_ge)
+        ts(W("Uf"), rows("b2", 0, 8), 1.5, None, A.is_ge)
+        for k in range(3): mm(X("b4", S(k, 12, 3)), W("I1"), W("Mf"), True, True)
+        one = X("ones", S(0, 256))
+        mm(rows("b2", 8, 16), W("I1"), one, True, False)
+        mm(rows("b2", 8, 16), W("Im1"), W("O"), False, False)
+        add("b2", 8, "Im1", "Mf", 0, 0)
+        add("b2", 12, "Im1", "Mf", 0, 0)
+        add("b2", 12, "Im1", "E", 4, 0)
+        add("b2", 12, "I1", "Uf", 4, 0, last=True)
+        tt(W("keys"), rows("b4", 0, 12), W("vk"), A.mult)
+        tt(rows("mz", 0, 4), X("b4", S(0, 12, 3)), rows(st, 4, 8), A.mult)
+        tt(rows("mz", 4, 8), X("b4", S(0, 12, 3)), rows(st, 8, 12), A.mult)
+        tt(W("t1"), X("keys", S(0, 2)), X("keys", S(2, 4)), A.max)
+        tt(W("vz"), rows("b2", 8, 16), rows(st, 8, 16), A.mult)
+        tt(W("t2"), X("t1", 0), X("t1", 1), A.max)
+        tt(W("uz"), rows("Uf", 0, 4), rows(st, 0, 4), A.mult)
+        tt(W("t3"), W("t2"), W("fall"), A.max)
+        ts(W("tv"), W("t3"), 8191, None, A.bitwise_and)
+        cp(W("hi"), X("tv", 0))
+        cp(X("own", 0), X("tv", 0))
+        tt(W("lw"), X("tv", 0), W("hi"), A.subtract)
+        cp(W("lgg"), X("tv", S(1, 3)))
+        def S_even(bank, base, sh):
+            add(bank, base, "J1", "oab", 0, sh)
+            add(bank, base, "J1", "oab", 12, sh - 1)
+            add(bank, base, "J1", "vz", 0, sh)
+            add(bank, base, "J1", "uz", 0, sh, last=True)
+        def S_odd(bank, base, sh):
+            add(bank, base, "J1", "oab", 4, sh)
+            add(bank, base, "J1", "oab", 8, sh)
+            add(bank, base, "J1", "vz", 4, sh, last=True)
+        de, do = (0, 1) if t == 0 else (-1, 0)
+        o1 = X("ones", S(0, 128))
+        def start(bank):
+            mm(rows(bank, 0, 4), W("cm2048"), o1, True, False)
+            mm(rows(bank, 0, 4), W("cp1"), o1, False, False)
+        start("b7"); start("b6")
+        if t < 2:
+            S_even("b7", 0, do); S_odd("b6", 0, de)
+        else:
+            S_even("b6", 0, 0); S_odd("b7", 0, 0)
+        def goals(lo, hi):
+            for j in range(lo, hi):
+                mm(X("b1", j), X("BB", j), W("hi"), True, False)
+                mm(X("b1", j), X("BB", j), W("lw"), False, True)
+        ec = [NB * (M * (e - 1) - e * (e - 1) // 2) for e in range(M + 1)]
+        def pairs(lo, hi):
+            tt(rows("eq", lo, hi), rows("b1", lo, hi), rows("own", lo, hi), A.is_equal)
+            for e in range(1, M):
+                tt(X("ee", S(lo, hi), S(ec[e], ec[e + 1])), X("b1", S(lo, hi), S(0, NB), S(0, M - e)), X("own", S(lo, hi), S(0, NB), S(e, M)), A.is_equal)
+        goals(0, 8)
+        for k in (1, 2, 4, 8): act(rows("own", k, 2 * k), rows("own", 0, k), F.Copy)
+        out = "po%d" % (t + 1)
+        if t < 2:
+            index_stage(out, "lo%d" % (t + 1), lambda: pairs(0, 8))
+            send(rank + 1, W("l%d" % (t + 1)), W("lo%d" % (t + 1)), "l%d" % (t + 1))
+        else:
+            for h in (0, 1): act(X("fog", S(0, 4), h), rows("b%d" % (6 + h), 0, 4), F.Identity, bias=2048.0, scale=-1.0)
+            send(rank - 2, W("fig"), W("fog"), "fg")
+            pairs(0, 8)
+        goals(8, 16)
+        mm(rows("b3", 4, 12), W("I1"), one, True, False)
+        mm(rows("b3", 4, 12), W("Im1"), W("O"), False, False)
+        mm(rows("b3", 4, 12), W("Im1"), W("Uf"), False, False)
+        add("b3", 4, "Im1", "O", 4, -1)
+        add("b3", 8, "Im1", "O", 0, 0)
+        add("b3", 8, "Im1", "Mf", 0, 0, last=True)
+        if t < 2:
+            for a in range(4): mm(rows("b3", 12, 13), W("SG"), rows("Mf", a, a + 1), a == 0, a == 3)
+        off = X("lgg", S(0, 64))
+        emit("s", lambda: s.activation(T.gab[:], T.win[:, 0:4096].indirect(off[0]), F.Copy), [X("win", S(0, 4096)), off], [W("gab")])
+        pe = X("b7", S(8, 10), S(0, NE // 2))
+        def count(lo, hi):
+            for j in range(lo, min(hi, 15)): mm(X("b2", 0), X("MK", j), X("eq", j), False, False)
+            for j in range(lo, hi): mm(pe, W("I1"), X("ee", j), j == 0, j == 15)
+        mm(X("b2", 0), W("I1"), W("hi"), True, False)
+        mm(X("b2", 0), W("I1"), W("lw"), False, False)
+        count(0, 8)
+        for h in (0, 1): mm(W("b4"), W("I1"), X("gab", S(512 * h, 512 * h + 512)), h == 0, False)
+        for h in (0, 1): mm(rows("b4", 8 * h, 8 * h + 8), W("cmh"), one, False, h == 1)
+        act(W("vf"), W("b4"), F.Identity, bias=8388608.0, scale=0.5)
+        act(W("vals"), W("vf"), F.Identity, bias=-8388608.0)
+        pairs(8, 16)
+        count(8, 16)
+        def memories():
+            tt(rows("kab", 0, 8), rows("b3", 4, 12), rows(st, 16, 24), A.mult)
+            tt(rows("kab", 8, 16), rows("b3", 4, 12), rows(st, 24, 32), A.mult)
+        def memory_sums():
+            for j, mzr in ((0, 4), (1, 0)):
+                ev, od = (4, 0) if t < 2 else (0, 4)
+                se, so = (do, de) if t < 2 else (0, 0)
+                for (a, b, c) in pieces(se):
+                    r = rows("b0", 8 * j + ev + a, 8 * j + ev + b)
+                    mm(r, W("J1"), rows("kab", 8 * j + c, 8 * j + c + b - a), True, False)
+                    mm(r, W("J1"), rows("mz", mzr + c, mzr + c + b - a), False, True)
+                for (a, b, c) in pieces(so):
+                    mm(rows("b0", 8 * j + od + a, 8 * j + od + b), W("J1"), rows("kab", 8 * j + 4 + c, 8 * j + 4 + c + b - a), True, True)
+            if t < 2:
+                act(rows(out, 16, 32), W("b0"), F.Copy)
+                act(rows(out, 32, 33), rows("b3", 12, 13), F.Copy)
+                send(rank + 1, rows("st%d" % (t + 1), 16, 33), rows(out, 16, 33), "s%db" % (t + 1))
+            else:
+                for j in (0, 1):
+                    for h in (0, 1): act(X("foab", j, S(0, 4), h), rows("b0", 8 * j + 4 * h, 8 * j + 4 * h + 4), F.Identity, bias=4095.0, scale=-1.0)
+                send(rank - 2, W("fiab"), W("foab"), "fab")
+        if t < 2:
+            index_rest(out)
+            send(rank + 1, rows("st%d" % (t + 1), 0, 16), rows(out, 0, 16), "s%da" % (t + 1))
+        memories()
+        cp(W("ce"), pe)
+        for e in range(1, M): mm(X("b2", 0, S(0, NB), S(e, M)), W("I8k"), X("ce", S(ec[e], ec[e + 1])), False, e == M - 1)
+        memory_sums()
+        tt(W("dm"), X("b2", 0), X("fall", 0), A.min)
+        cp(W("dst"), W("dm"))
+        for q in range(NB - 1, -1, -1):
+            off2, va, wn = X("dst", S(q * M, q * M + M)), X("vals", S(16 * M * q, 16 * M * (q + 1))), W("win")
+            emit("v", lambda: v.tensor_copy(T.win[:, 0:4608].indirect(off2[0]), va[0]), [off2, va], [wn])
+
+    for t in range(3): visit(t)
+    cp(X("win", S(4095, 4096)), X("sv", S(0, 1)))
+    dma("y", T.ox[:], T.win[:, 0:4096], [X("win", S(0, 4096))], [])
+    dma("s", T.og[:], T.fig[:], [W("fig")], [])
+    dma("s", T.oa[:], T.fiab[:, 0], [X("fiab", 0)], [])
+    dma("y", T.ob[:], T.fiab[:, 1], [X("fiab", 1)], [])
+    for sem in cnt: g.wait_ge(T.sem[sem], cnt[sem])

@@ -4,7 +4,7 @@ from concourse.mybir import AluOpType as A, ActivationFunctionType as F
 M = 4
 NB = 32 // M
 NE = NB * M * (M - 1) // 2
-f32, bf, i32, u16 = "float32", "bfloat16", "int32", "uint16"
+f32, f16, bf, i32, u16 = "float32", "float16", "bfloat16", "int32", "uint16"
 SCRATCH = {
     "win": ("sbuf", [128, 4608], bf), "sv": ("sbuf", [128, 16], bf),
     "yv0": ("sbuf", [128, 1024], bf), "yv1": ("sbuf", [128, 1024], bf), "yv2": ("sbuf", [128, 1024], bf),
@@ -16,22 +16,24 @@ SCRATCH = {
     "lo1": ("sbuf", [128, 384], u16), "lo2": ("sbuf", [128, 384], u16),
     "dd": ("sbuf", [128, 6144], bf), "ab": ("sbuf", [128, 6144], bf),
     "E": ("sbuf", [128, 8, 32], bf), "AE": ("sbuf", [128, 8, 32], bf), "O": ("sbuf", [128, 8, 32], bf),
-    "UX": ("sbuf", [128, 8, 32], bf), "Mf": ("sbuf", [128, 4, 32], bf), "Uf": ("sbuf", [128, 8, 32], bf),
+    "UX": ("sbuf", [128, 8, 32], bf), "Mf": ("sbuf", [128, 4, 32], bf),
     "Eo": ("sbuf", [128, 4, 32], bf), "Cb": ("sbuf", [128, 1, 32], bf),
     "thr": ("sbuf", [128, 8, 32], f32), "dsb": ("sbuf", [128, 8, 32], f32), "mn": ("sbuf", [128, 4, 32], f32),
-    "vk": ("sbuf", [128, 4, 3, 32], f32), "keys": ("sbuf", [128, 4, 3, 32], f32), "t1": ("sbuf", [128, 2, 3, 32], f32),
-    "t2": ("sbuf", [128, 3, 32], f32), "fall": ("sbuf", [128, 3, 32], f32), "t3": ("sbuf", [128, 3, 32], i32),
-    "tv": ("sbuf", [128, 3, 32], i32), "lgg": ("sbuf", [128, 64], u16), "hi": ("sbuf", [128, 32], bf),
+    "nv": ("sbuf", [128, 12, 32], f32), "keys": ("sbuf", [128, 12, 32], f16), "fall": ("sbuf", [128, 32], f32),
+    "fallc": ("sbuf", [128, 32], f32), "code": ("sbuf", [128, 32], f16), "BH": ("sbuf", [128, 16, 128], f16), "IH": ("sbuf", [128, 128], f16),
+    "Kb": ("sbuf", [128, 8, 32], bf),
+    "xg": ("sbuf", [128, 512], bf), "zz": ("sbuf", [128, 16, 128], bf), "Tf": ("sbuf", [128, 8, 32], bf), "Ff": ("sbuf", [128, 4, 32], bf), "lgg": ("sbuf", [128, 64], u16), "hi": ("sbuf", [128, 32], bf),
     "lw": ("sbuf", [128, 32], bf), "own": ("sbuf", [128, 16, NB, M], f32), "eq": ("sbuf", [128, 16, 32], bf), "ee": ("sbuf", [128, 16, NE], bf), "ce": ("sbuf", [128, NE], bf),
     "gab": ("sbuf", [128, 1024], bf), "vf": ("sbuf", [128, 512], f32), "vals": ("sbuf", [128, 512], bf), "dm": ("sbuf", [128, 32], i32),
     "dst": ("sbuf", [128, 32], u16),
-    "oab": ("sbuf", [128, 16, 32], f32), "kab": ("sbuf", [128, 16, 32], f32), "mz": ("sbuf", [128, 8, 32], f32),
-    "uz": ("sbuf", [128, 4, 32], f32), "vz": ("sbuf", [128, 8, 32], f32), "X": ("sbuf", [128, 8, 32], f32),
+    "oab": ("sbuf", [128, 16, 32], f16), "kab": ("sbuf", [128, 16, 32], f16), "mz": ("sbuf", [128, 8, 32], f16),
+    "vz": ("sbuf", [128, 12, 32], f16), "X": ("sbuf", [128, 8, 32], f32),
     "P": ("sbuf", [128, 8, 32], i32), "H": ("sbuf", [128, 8, 32], i32), "NQ": ("sbuf", [128, 8, 32], i32),
     "IDX": ("sbuf", [128, 8, 32], i32),
-    "fog": ("sbuf", [128, 4, 2, 32], f32), "foab": ("sbuf", [128, 2, 4, 2, 32], f32),
-    "fig": ("sbuf", [128, 4, 2, 32], f32), "fiab": ("sbuf", [128, 2, 4, 2, 32], f32),
-    "ones": ("sbuf", [128, 256], bf), "SS": ("sbuf", [128, 2048], bf), "BB": ("sbuf", [128, 16, 128], bf),
+    "fog": ("sbuf", [128, 8, 32], u16), "foab": ("sbuf", [128, 16, 32], u16),
+    "fig": ("sbuf", [128, 8, 32], u16), "fiab": ("sbuf", [128, 16, 32], u16),
+    "og_": ("sbuf", [128, 4, 2, 32], f32), "oa_": ("sbuf", [128, 4, 2, 32], f32), "ob_": ("sbuf", [128, 4, 2, 32], f32),
+    "ones": ("sbuf", [128, 256], bf), "on5": ("sbuf", [128, 512], bf), "SS": ("sbuf", [128, 2048], bf), "BB": ("sbuf", [128, 16, 128], bf),
     "MK": ("sbuf", [128, 16, 128], bf), "SG": ("sbuf", [128, 128], bf),
     "pi": ("sbuf", [128, 1], i32), "pa": ("sbuf", [128, 1], i32), "pb": ("sbuf", [128, 1], i32),
     "pm": ("sbuf", [128, 1], f32), "pg": ("sbuf", [128, 1], f32), "io8": ("sbuf", [128, 8], f32),
@@ -39,16 +41,17 @@ SCRATCH = {
 }
 for _n in ("st0", "st1", "st2", "po1", "po2"):
     SCRATCH[_n] = ("sbuf", [128, 33, 32], f32)
-WB = {"I1": 1, "Im1": -1, "I2": 2, "Im2": -2, "I8k": 8192, "I16k": 16384, "Im16k": -16384, "I1920": 1920, "I28": 28}
+WB = {"I1": 1, "Im1": -1, "I8k": 8192, "Im8k": -8192, "I16k": 16384, "Im16k": -16384, "I1920": 1920, "I28": 28, "I2k": 2048, "Im2k": -2048}
 WF = {"J1": 1, "Jm1": -1, "Jm101": -101, "Jm129": -129}
-CM = {"c230": -230 / 128, "cm1": -1 / 128, "cm2048": -16, "cp1": 1 / 128, "cmh": -0.5 / 128}
+CM = {"c230": -230 / 128, "cm1": -1 / 128, "c2k": 16.0, "cp1": 1 / 128, "cmh": -0.5 / 128, "c8k": 64.0}
 for _n in WB: SCRATCH[_n] = ("sbuf", [128, 128], bf)
 for _n in WF: SCRATCH[_n] = ("sbuf", [128, 128], f32)
 for _n in CM: SCRATCH[_n] = ("sbuf", [128, 128], bf)
 for _n in ("b0", "b3", "b4", "b5", "b6", "b7"): SCRATCH[_n] = ("psum", [128, 16, 32], f32)
 for _n in ("b1", "b2"): SCRATCH[_n] = ("psum", [128, 16, NB, M], f32)
 NDMA = 16
-ARR = ["yi1", "yi2", "ti1", "ti2", "l1", "l2", "s1a", "s1b", "s2a", "s2b", "fg", "fab"]
+HELP = True
+ARR = ["yi1", "yi2", "ti1", "ti2", "l1", "l2", "s1a", "s1b", "s1c", "s2a", "s2b", "s2c", "fg", "fab"]
 SEMAPHORES = ["qv", "qs", "qt", "qg", "loc"] + ["d%d" % k for k in range(NDMA)] + ["a_" + n for n in ARR]
 _cache = {}
 
@@ -152,14 +155,19 @@ def rank_program(g, core, T, topo):
     for k in (0, 1, 2):
         if k == 1:
             for n, src in (("an", T.al), ("bn", T.bl), ("tn", T.th)): dma("y", T[n][:], src[:], [], [W(n)])
-        for h in (0, 1):
+        for h in (0, 1)[:2 if k == 0 else 1]:
             n = "yv%d" % k
             dma("y", T[n][:, h * 512:h * 512 + 512], T.yv[:, k * 512:k * 512 + 512], [], [X(n, S(h * 512, h * 512 + 512))])
-    for n, k in (("yi1", 1), ("ti1", 1), ("yi2", 2), ("ti2", 2)): arrives(rank - k, n, W(n))
+    for k in (1, 2):
+        arrives(rank - k, "yi%d" % k, X("yi%d" % k, S(0, 512)))
+        arrives(rank - k, "ti%d" % k, W("ti%d" % k))
+        n = T["yi%d" % k]
+        dma("y", n[:, 512:1024], n[:, 0:512], [X("yi%d" % k, S(0, 512))], [X("yi%d" % k, S(512, 1024))])
     for k in (1, 2):
         arrives(rank - 1, "l%d" % k, W("l%d" % k))
-        arrives(rank - 1, "s%da" % k, rows("st%d" % k, 0, 16))
-        arrives(rank - 1, "s%db" % k, rows("st%d" % k, 16, 33))
+        arrives(rank - 1, "s%da" % k, rows("st%d" % k, 0, 8))
+        arrives(rank - 1, "s%db" % k, rows("st%d" % k, 24, 33))
+        arrives(rank - 1, "s%dc" % k, rows("st%d" % k, 8, 24))
     arrives(rank + 2, "fg", W("fig")); arrives(rank + 2, "fab", W("fiab"))
 
     emit("g", lambda: g.iota(T.pi[:], [[0, 1]], 0, 1), [], [W("pi")])
@@ -168,21 +176,20 @@ def rank_program(g, core, T, topo):
     emit("g", lambda: g.affine_select(T.I1[:], T.ones[:, 0:128], [[-1, 128]], A.is_equal, 0.0, 0, 1), [X("ones", S(0, 128))], [W("I1")])
     emit("g", lambda: g.iota(T.io8[:], [[1, 8]], 0, 0, **big), [], [W("io8")])
     emit("g", lambda: g.iota(T.iop[:], [[0, 8], [1, 16]], 0, 0, **big), [], [W("iop")])
-    emit("g", lambda: g.iota(T.ioi[:], [[16, 32]], 4096, 0, **big), [], [W("ioi")])
-    ms(W("SS"), 0.0)
+    emit("g", lambda: g.iota(T.ioi[:], [[16, 32]], 2048, 0, **big), [], [W("ioi")])
+    ms(W("zz"), 0.0)
+    emit("g", lambda: g.affine_select(T.BB[:], T.zz[:], [[-1, 16], [-16, 8], [0, 16]], A.not_equal, 1.0, 0, 1), [W("zz")], [W("BB")])
     for n in CM: ms(W(n), CM[n])
     ts(W("pa"), W("pi"), 15, None, A.bitwise_and)
     ts(W("pb"), W("pi"), 4, None, A.arith_shift_right)
     cp(W("pm"), W("pa")); cp(W("pg"), W("pb"))
     ts(W("bm8"), W("io8"), W("pg"), None, A.is_equal)
     ts(W("SG"), W("iop"), W("pm"), None, A.is_equal)
-    ms(X("fall", S(1, 3)), 0.0)
-    ts(X("fall", 0), W("ioi"), W("pm"), None, A.add)
+    ts(W("fall"), W("ioi"), W("pm"), None, A.add)
+    ts(W("fallc"), W("fall"), 2.0, -2046.0, A.mult, A.add)
+    cp(W("IH"), W("I1"))
     for n in ("J1", "Jm1", "Jm101", "Jm129"): act(W(n), W("I1"), F.Identity, scale=float(WF[n]))
     for n in ("I1920", "I28"): act(W(n), W("I1"), F.Identity, scale=float(WB[n]))
-    for e in range(8):
-        act(X("SS", S(16 * e, 16 * e + 129 * 15 + 1, 129)), X("ones", S(0, 16)), F.Identity, scale=X("bm8", S(e, e + 1)))
-    for n in ("Im1", "I2", "Im2", "I8k", "I16k", "Im16k"): act(W(n), W("I1"), F.Identity, scale=float(WB[n]))
 
     def pieces(sh): return {0: [(0, 4, 0)], 1: [(0, 3, 1), (3, 4, 0)], -1: [(1, 4, 0), (0, 1, 3)]}[sh]
     def add(bank, base, w, src, sbase, sh, first=False, last=False):
@@ -190,51 +197,58 @@ def rank_program(g, core, T, topo):
         for j, (a, b, c) in enumerate(ps):
             mm(rows(bank, base + a, base + b), W(w), rows(src, sbase + c, sbase + c + b - a), first and j == 0, last and j == len(ps) - 1)
 
-    def index_stage(po, lo, meanwhile=None):
+    def index_stage(po, lo, meanwhile=None, goals=None, pair=None):
         ts(rows("X", 4, 8), rows("b7", 0, 4), -2047.0, -4127.0, A.is_equal, A.mult)
-        act(rows(po, 4, 8), rows("b7", 0, 4), F.Identity, bias=2047.0)
+        act(rows(po, 0, 4), rows("b7", 0, 4), F.Identity, bias=-1.0)
         act(W("Eo"), rows("b7", 0, 4), F.Relu, bias=-2046.0, scale=-1.0)
         ts(X(lo, S(0, 128)), rows("b6", 0, 4), -1.0, 2048.0, A.mult, A.add)
-        ts(rows("X", 0, 4), rows("b6", 0, 4), 2048.0, None, A.add)
         tt(rows("P", 4, 7), rows("X", 4, 7), rows("b6", 1, 4), A.mult)
         tt(rows("P", 7, 8), rows("X", 7, 8), rows("b6", 0, 1), A.mult)
-        act(rows(po, 8, 12), rows("b6", 0, 4), F.Identity, bias=2047.0)
+        act(rows("X", 0, 4), rows("b6", 0, 4), F.Identity, bias=2048.0)
+        act(rows(po, 4, 8), rows("b6", 0, 4), F.Identity, bias=-1.0)
+        if meanwhile: meanwhile()
         tt(rows("P", 0, 4), rows("X", 0, 4), rows("b7", 0, 4), A.mult)
         one = X("ones", S(0, 128))
         mm(rows("b5", 4, 8), W("cm1"), one, True, False)
-        add("b5", 4, "Jm1", po, 4, 0)
+        mm(rows("b5", 4, 8), W("c2k"), one, False, False)
+        add("b5", 4, "Jm1", po, 0, 0)
         add("b5", 4, "I1920", "Eo", 0, 0)
         add("b5", 4, "I28", "Eo", 0, 0, last=True)
         mm(rows("b5", 0, 4), W("c230"), one, True, False)
-        add("b5", 0, "Jm129", po, 4, 0)
-        add("b5", 0, "Jm101", po, 8, 0, last=True)
+        add("b5", 0, "Jm129", po, 0, 0)
+        add("b5", 0, "Jm101", po, 4, 0, last=True)
         ts(W("H"), W("P"), 5, None, A.arith_shift_right)
-        if meanwhile: meanwhile()
+        if goals: goals()
         tt(W("NQ"), W("H"), rows("b5", 0, 8), A.add)
         ts(W("IDX"), W("NQ"), 4095, None, A.bitwise_and)
+        if pair: pair(3)
         cp(X(lo, S(128, 384)), W("IDX"))
 
     def index_rest(po):
-        ts(rows(po, 0, 4), rows("IDX", 0, 4), -1.0, 4095.0, A.mult, A.add)
-        ts(rows(po, 12, 16), rows("IDX", 4, 8), -1.0, 4095.0, A.mult, A.add)
+        ts(rows(po, 8, 16), W("IDX"), -1.0, 2047.0, A.mult, A.add)
 
     for h in (0, 1): ts(rows("b%d" % (6 + h), 0, 4), X("gn", S(0, 4), h), -1.0, 2048.0, A.mult, A.add)
     index_stage("st0", "l0")
-    index_rest("st0")
-    ms(W("BB"), 1.0); ms(W("MK"), 8192.0)
+    act(W("SS"), W("zz"), F.Copy)
+    for e in range(8):
+        act(X("SS", S(16 * e, 16 * e + 129 * 15 + 1, 129)), X("ones", S(0, 16)), F.Identity, scale=X("bm8", S(e, e + 1)))
+    for n in ("Im1", "I8k", "Im8k", "I16k", "Im16k", "I2k", "Im2k"): act(W(n), W("I1"), F.Identity, scale=float(WB[n]))
     def home_rest():
-        for n, b in (("an", 16), ("bn", 24)):
-            for h in (0, 1): ts(rows("st0", b + 4 * h, b + 4 * h + 4), X(n, S(0, 4), h), -1.0, 4095.0, A.mult, A.add)
+        index_rest("st0")
+        for n, b in (("an", 24), ("bn", 16)):
+            for h in (0, 1): ts(rows("st0", b + 4 * h, b + 4 * h + 4), X(n, S(0, 4), h), -1.0, 2047.0, A.mult, A.add)
         for h in (0, 1): cp(rows("tf0", 4 * h, 4 * h + 4), X("tn", S(0, 4), h))
         for k in (1, 2): send(rank + k, W("ti%d" % k), W("tf0"), "ti%d" % k)
-    for k in (1, 2): send(rank + k, W("yi%d" % k), W("yv%d" % k), "yi%d" % k)
-    emit("g", lambda: g.affine_select(T.BB[:], T.BB[:], [[-1, 16], [-16, 8], [0, 16]], A.is_equal, 0.0, 0, 1), [W("BB")], [W("BB")])
-    emit("g", lambda: g.affine_select(T.MK[:], T.MK[:], [[0, 16], [-16, 8], [-1, 16]], A.is_equal, 0.0, 0, 1), [W("MK")], [W("MK")])
-    emit("g", lambda: g.affine_select(T.MK[:], T.MK[:], [[-1, 16], [0, 8], [1, 16]], A.is_gt, 0.0, 0, 0), [W("MK")], [W("MK")])
+    for k in (1, 2): send(rank + k, X("yi%d" % k, S(0, 512)), X("yv%d" % k, S(0, 512)), "yi%d" % k)
+    def goal_constants():
+        act(W("on5"), X("zz", S(0, 4)), F.Identity, bias=1.0)
+        emit("g", lambda: g.affine_select(T.MK[:], T.zz[:], [[0, 16], [-16, 8], [-1, 16]], A.not_equal, 8192.0, 0, 1), [W("zz")], [W("MK")])
+        emit("g", lambda: g.affine_select(T.MK[:], T.MK[:], [[-1, 16], [0, 8], [1, 16]], A.is_gt, 0.0, 0, 0), [W("MK")], [W("MK")])
+    cp(W("BH"), W("BB"))
     cp(X("sv", S(0, 1)), X("win", S(4095, 4096)))
     ms(X("win", S(4095, 4096)), 512.0)
 
-    CALLS = [(0, 64), (64, 64), (256, 64), (320, 64), (128, 64), (192, 32), (224, 32)]
+    CALLS = [(0, 64), (64, 64), (256, 64), (320, 64), (128, 64), (192, 32 if HELP else 64)]
     def visit(t):
         st, ls, yv, th = "st%d" % t, "l%d" % t, ("yi%d" % t if t else "yv0"), ("ti%d" % t if t else "tf0")
 
@@ -249,170 +263,202 @@ def rank_program(g, core, T, topo):
                 mm(rows(bank, r0, r0 + n // 32), X("SS", S(128 * j, 128 * j + 128)), X("ab", S(16 * c + j, 16 * c + 16 * n, 16)),
                    j == 0 and bank == "b0", j == 15 and (bank == "b0" or c == 192))
         def prep_a():
-            act(rows("E", 0, 4), rows(st, 8, 12), F.Relu, bias=1.0, scale=-1.0)
-            act(rows("E", 4, 8), rows(st, 4, 8), F.Relu, bias=1.0, scale=-1.0)
-            for a in range(4):
-                act(X("vk", a), X(st, S(a, 12, 4)), F.Identity, bias=float(4095 + 8192 * (4 - a)), scale=-1.0)
-        def prep_b():
-            act(W("AE"), rows(st, 16, 24), F.Relu, bias=1.0, scale=-1.0)
-            if t: act(W("Cb"), rows(st, 32, 33), F.Copy)
+            act(rows("E", 0, 4), rows(st, 4, 8), F.Relu, bias=-2047.0, scale=-1.0)
+            act(rows("E", 4, 8), rows(st, 0, 4), F.Relu, bias=-2047.0, scale=-1.0)
             mm(rows("b6", 0, 8), W("I16k"), rows("E", 0, 8), True, False)
-            mm(rows("b6", 0, 8), W("I16k"), rows("AE", 0, 8), False, False)
             add("b6", 0, "Im16k", "E", 4, 0)
             add("b6", 4, "Im16k", "E", 0, 1)
             if t == 1:
                 add("b6", 0, "J1", th, 4, 0); add("b6", 4, "J1", th, 0, 1)
             else:
-                mm(rows("b6", 0, 8), W("J1"), rows(th, 0, 8), False, t == 0)
+                mm(rows("b6", 0, 8), W("J1"), rows(th, 0, 8), False, False)
+        def prep_b():
+            act(W("AE"), rows(st, 24, 32), F.Relu, bias=-2047.0, scale=-1.0)
+            if t: act(W("Cb"), rows(st, 32, 33), F.Copy)
+            mm(rows("b6", 0, 8), W("I16k"), rows("AE", 0, 8), False, t == 0)
             if t:
                 for k in range(8): mm(rows("b6", k, k + 1), W("I1"), W("Cb"), False, k == 7)
 
+        one, o1 = X("ones", S(0, 256)), X("ones", S(0, 128))
+        def empty_gates():
+            mm(rows("b3", 0, 4), W("Im1"), rows("E", 0, 4), True, False)
+            mm(rows("b2", 0, 8), W("I1"), W("E"), True, False)
+            add("b2", 4, "Im1", "E", 0, 1)
+            mm(rows("b4", 0, 12), W("I1"), X("zz", S(0, 3)), True, False)
+            mm(rows("b4", 0, 4), W("I1"), o1, False, False)
+            mm(rows("b4", 8, 12), W("I1"), o1, False, False)
+            add("b4", 8, "Im1", "E", 4, 0)
+        def open_gates():
+            add("b3", 0, "Im1", "O", 4, 0)
+            add("b2", 0, "Im1", "O", 4, -1)
+            add("b2", 4, "Im1", "O", 0, 0)
+            add("b4", 0, "Im1", "O", 0, 0)
+            add("b4", 8, "Im1", "O", 4, 0)
+        de, do = (0, 1) if t == 0 else (-1, 0) if t == 1 else (0, 0)
+        be, bo = ("b7", "b6") if t < 2 else ("b6", "b7")
+        def places_0():
+            for bank in (be, bo):
+                mm(rows(bank, 0, 4), W("cp1"), o1, True, False)
+        def places_e():
+            add(be, 0, "IH", "oab", 8, do)
+            add(be, 0, "IH", "oab", 4, do - 1)
+            add(be, 0, "I2k", "O", 4, do - 1)
+        def places_o():
+            add(bo, 0, "IH", "oab", 12, de)
+            add(bo, 0, "IH", "oab", 0, de)
+            add(bo, 0, "I2k", "O", 0, de)
+            add(bo, 0, "Im2k", "E", 4, de)
+        if HELP:
+            off0 = X(ls, S(224, 256))
+            emit("s", lambda: s.activation(T.xg[:], T.win[:, 0:4096].indirect(off0[0]), F.Copy), [X("win", S(0, 4096)), off0], [W("xg")])
         for k, (c, n) in enumerate(CALLS):
             gather(c, n)
-            if k == 1 and t == 0: home_rest()
-        for k, (c, n) in enumerate(CALLS):
-            size(c, n)
-            if k == 1: prep_a()
-            if k == 2: prep_b()
+            if k == 1 and t == 0:
+                home_rest()
+                goal_constants()
             if k == 4:
+                tt(W("O"), rows("b0", 0, 8), W("thr"), A.is_gt)
+                mm(rows("b5", 0, 8), W("I1"), W("O"), True, True)
+                mm(rows("b5", 8, 16), W("I1"), W("O"), True, True)
+            if k == len(CALLS) - 1: tt(W("oab"), W("b5"), rows(st, 16, 32), A.mult)
+            if k == 3: prep_b()
+            size(c, n)
+            if k == 2: prep_a()
+            if k == 4:
+                act(W("dsb"), rows("b0", 0, 8), F.Copy)
                 mm(rows("b1", 0, 4), W("I8k"), rows("E", 4, 8), True, False)
-                act(W("thr"), rows("b6", 0, 8), F.Identity, bias=16384.0)
+            if k == 0 and HELP:
+                mm(W("b4"), W("I1"), W("xg"), True, False)
+                mm(W("b4"), W("Im1"), X(yv, S(0, 512)), False, True)
+            if k == 1 and HELP: act(X("ab", S(16 * 224, 16 * 256)), W("b4"), F.Abs)
             if k < 5: total(c, n)
-            if k == 6: total(192, 64)
-        tt(W("O"), rows("b0", 0, 8), W("thr"), A.is_gt)
-        act(W("dsb"), rows("b0", 0, 8), F.Copy)
+            if k == 3:
+                act(W("thr"), rows("b6", 0, 8), F.Identity, bias=16384.0)
+                empty_gates()
+            if k == 4: open_gates()
+        act(W("nv"), rows(st, 0, 12), F.Identity, bias=-1.0, scale=-1.0)
+        total(192, 64)
+        places_0()
         tt(W("mn"), rows("b0", 0, 4), rows("dsb", 4, 8), A.min)
         tt(rows("UX", 4, 7), rows("b0", 4, 7), rows("dsb", 1, 4), A.is_lt)
         tt(rows("UX", 7, 8), rows("b0", 7, 8), rows("dsb", 0, 1), A.is_lt)
-        mm(rows("b5", 0, 8), W("I1"), W("O"), True, True)
-        mm(rows("b5", 8, 16), W("I1"), W("O"), True, True)
-        mm(rows("b3", 0, 4), W("Im1"), rows("E", 0, 4), True, False)
-        add("b3", 0, "Im1", "O", 4, 0)
-        mm(rows("b2", 0, 8), W("I1"), W("E"), True, False)
-        add("b2", 0, "Im1", "O", 4, 0)
-        add("b2", 0, "Im2", "O", 4, -1)
-        add("b2", 4, "Im1", "O", 0, 0)
-        add("b2", 4, "Im1", "E", 0, 1)
         add("b2", 4, "I1", "UX", 4, 0)
         tt(rows("UX", 0, 4), rows("b1", 0, 4), W("mn"), A.is_lt)
-        tt(W("oab"), W("b5"), rows(st, 16, 32), A.mult)
         add("b3", 0, "I1", "UX", 0, 0, last=True)
-        add("b2", 0, "I2", "UX", 0, 0, last=True)
-        ts(W("Mf"), rows("b3", 0, 4), 0.5, None, A.is_ge)
-        ts(W("Uf"), rows("b2", 0, 8), 1.5, None, A.is_ge)
-        for k in range(3): mm(X("b4", S(k, 12, 3)), W("I1"), W("Mf"), True, True)
-        one = X("ones", S(0, 256))
-        mm(rows("b2", 8, 16), W("I1"), one, True, False)
-        mm(rows("b2", 8, 16), W("Im1"), W("O"), False, False)
-        add("b2", 8, "Im1", "Mf", 0, 0)
-        add("b2", 12, "Im1", "Mf", 0, 0)
-        add("b2", 12, "Im1", "E", 4, 0)
-        add("b2", 12, "I1", "Uf", 4, 0, last=True)
-        tt(W("keys"), rows("b4", 0, 12), W("vk"), A.mult)
-        tt(rows("mz", 0, 4), X("b4", S(0, 12, 3)), rows(st, 4, 8), A.mult)
-        tt(rows("mz", 4, 8), X("b4", S(0, 12, 3)), rows(st, 8, 12), A.mult)
-        tt(W("t1"), X("keys", S(0, 2)), X("keys", S(2, 4)), A.max)
-        tt(W("vz"), rows("b2", 8, 16), rows(st, 8, 16), A.mult)
-        tt(W("t2"), X("t1", 0), X("t1", 1), A.max)
-        tt(W("uz"), rows("Uf", 0, 4), rows(st, 0, 4), A.mult)
-        tt(W("t3"), W("t2"), W("fall"), A.max)
-        ts(W("tv"), W("t3"), 8191, None, A.bitwise_and)
-        cp(W("hi"), X("tv", 0))
-        cp(X("own", 0), X("tv", 0))
-        tt(W("lw"), X("tv", 0), W("hi"), A.subtract)
-        cp(W("lgg"), X("tv", S(1, 3)))
-        def S_even(bank, base, sh):
-            add(bank, base, "J1", "oab", 0, sh)
-            add(bank, base, "J1", "oab", 12, sh - 1)
-            add(bank, base, "J1", "vz", 0, sh)
-            add(bank, base, "J1", "uz", 0, sh, last=True)
-        def S_odd(bank, base, sh):
-            add(bank, base, "J1", "oab", 4, sh)
-            add(bank, base, "J1", "oab", 8, sh)
-            add(bank, base, "J1", "vz", 4, sh, last=True)
-        de, do = (0, 1) if t == 0 else (-1, 0)
-        o1 = X("ones", S(0, 128))
-        def start(bank):
-            mm(rows(bank, 0, 4), W("cm2048"), o1, True, False)
-            mm(rows(bank, 0, 4), W("cp1"), o1, False, False)
-        start("b7"); start("b6")
-        if t < 2:
-            S_even("b7", 0, do); S_odd("b6", 0, de)
-        else:
-            S_even("b6", 0, 0); S_odd("b7", 0, 0)
-        def goals(lo, hi):
-            for j in range(lo, hi):
-                mm(X("b1", j), X("BB", j), W("hi"), True, False)
-                mm(X("b1", j), X("BB", j), W("lw"), False, True)
-        ec = [NB * (M * (e - 1) - e * (e - 1) // 2) for e in range(M + 1)]
-        def pairs(lo, hi):
-            tt(rows("eq", lo, hi), rows("b1", lo, hi), rows("own", lo, hi), A.is_equal)
-            for e in range(1, M):
-                tt(X("ee", S(lo, hi), S(ec[e], ec[e + 1])), X("b1", S(lo, hi), S(0, NB), S(0, M - e)), X("own", S(lo, hi), S(0, NB), S(e, M)), A.is_equal)
-        goals(0, 8)
-        for k in (1, 2, 4, 8): act(rows("own", k, 2 * k), rows("own", 0, k), F.Copy)
-        out = "po%d" % (t + 1)
-        if t < 2:
-            index_stage(out, "lo%d" % (t + 1), lambda: pairs(0, 8))
-            send(rank + 1, W("l%d" % (t + 1)), W("lo%d" % (t + 1)), "l%d" % (t + 1))
-        else:
-            for h in (0, 1): act(X("fog", S(0, 4), h), rows("b%d" % (6 + h), 0, 4), F.Identity, bias=2048.0, scale=-1.0)
-            send(rank - 2, W("fig"), W("fog"), "fg")
-            pairs(0, 8)
-        goals(8, 16)
-        mm(rows("b3", 4, 12), W("I1"), one, True, False)
-        mm(rows("b3", 4, 12), W("Im1"), W("O"), False, False)
-        mm(rows("b3", 4, 12), W("Im1"), W("Uf"), False, False)
-        add("b3", 4, "Im1", "O", 4, -1)
-        add("b3", 8, "Im1", "O", 0, 0)
-        add("b3", 8, "Im1", "Mf", 0, 0, last=True)
-        if t < 2:
-            for a in range(4): mm(rows("b3", 12, 13), W("SG"), rows("Mf", a, a + 1), a == 0, a == 3)
-        off = X("lgg", S(0, 64))
-        emit("s", lambda: s.activation(T.gab[:], T.win[:, 0:4096].indirect(off[0]), F.Copy), [X("win", S(0, 4096)), off], [W("gab")])
-        pe = X("b7", S(8, 10), S(0, NE // 2))
-        def count(lo, hi):
-            for j in range(lo, min(hi, 15)): mm(X("b2", 0), X("MK", j), X("eq", j), False, False)
-            for j in range(lo, hi): mm(pe, W("I1"), X("ee", j), j == 0, j == 15)
-        mm(X("b2", 0), W("I1"), W("hi"), True, False)
-        mm(X("b2", 0), W("I1"), W("lw"), False, False)
-        count(0, 8)
-        for h in (0, 1): mm(W("b4"), W("I1"), X("gab", S(512 * h, 512 * h + 512)), h == 0, False)
-        for h in (0, 1): mm(rows("b4", 8 * h, 8 * h + 8), W("cmh"), one, False, h == 1)
-        act(W("vf"), W("b4"), F.Identity, bias=8388608.0, scale=0.5)
-        act(W("vals"), W("vf"), F.Identity, bias=-8388608.0)
-        pairs(8, 16)
-        count(8, 16)
+        add("b2", 0, "I1", "UX", 0, 0, last=True)
+        ts(W("Mf"), rows("b3", 0, 4), 0.0, None, A.max)
+        act(W("Tf"), rows("b2", 0, 8), F.Relu, bias=-1.0)
+        if t < 2: places_e()
+        mm(rows("b3", 4, 8), W("I1"), W("Mf"), True, False)
+        for k in (1, 2, 3): mm(rows("b3", 4 + k, 8), W("Im1"), rows("Mf", 0, 4 - k), False, k == 3)
+        act(W("Ff"), rows("b3", 4, 8), F.Relu)
+        add("b4", 0, "Im1", "Mf", 0, 0)
+        add("b4", 4, "I1", "Mf", 0, 0)
+        add("b4", 8, "Im1", "Mf", 0, 0)
+        mm(rows("b4", 4, 12), W("I1"), W("Tf"), False, True)
+        if t < 2: places_o()
+        for k in range(3): mm(rows("b2", 4 * k, 4 * k + 4), W("I1"), W("Ff"), True, True)
+        for k in range(2): mm(rows("b5", 8 + 4 * k, 12 + 4 * k), W("I1"), W("Mf"), True, True)
+        tt(W("vz"), rows("b4", 0, 12), rows(st, 4, 16), A.mult)
+        tt(W("keys"), rows("b2", 0, 12), W("nv"), A.mult)
+        def places_b():
+            add(be, 0, "I2k", "Tf", 0, do)
+            add(bo, 0, "I2k", "Tf", 4, de)
+            add(bo, 0, "Im2k", "Mf", 0, de)
+            add(be, 0, "IH", "vz", 0, do)
+            add(be, 0, "IH", "vz", 4, do, last=True)
+            add(bo, 0, "IH", "vz", 8, de, last=True)
+        if t < 2: places_b()
+        for a in range(4): mm(rows("b3", 8, 11), W("IH"), X("keys", S(a, 12, 4)), a == 0, False)
+        mm(rows("b3", 10, 11), W("c8k"), X("ones", S(0, 32)), False, False)
+        for a in range(4): mm(rows("b3", 10, 11), W("Im8k"), rows("Ff", a, a + 1), False, a == 3)
+        def first_goals():
+            tt(W("code"), rows("b3", 10, 11), W("fallc"), A.min)
+            for k in range(4): tt(X("own", k), rows("b3", 10, 11), W("fallc"), A.min)
+            ts(W("lgg"), rows("b3", 8, 10), 2048.0, None, A.add)
+            for k in (4, 8): act(rows("own", k, 2 * k), rows("own", 0, k), F.Copy)
+        def keeps():
+            mm(rows("b3", 4, 12), W("I1"), one, True, False)
+            mm(rows("b3", 4, 12), W("Im1"), W("O"), False, False)
+            mm(rows("b3", 4, 12), W("Im1"), W("Tf"), False, False)
+            add("b3", 4, "Im1", "Mf", 0, 0)
+            add("b3", 4, "Im1", "O", 4, -1)
+            add("b3", 8, "Im1", "O", 0, 0)
+            add("b3", 8, "Im1", "Mf", 0, 0, last=True)
+            if t < 2:
+                for a in range(4): mm(rows("b3", 12, 13), W("SG"), rows("Mf", a, a + 1), a == 0, a == 3)
         def memories():
             tt(rows("kab", 0, 8), rows("b3", 4, 12), rows(st, 16, 24), A.mult)
             tt(rows("kab", 8, 16), rows("b3", 4, 12), rows(st, 24, 32), A.mult)
+            tt(rows("mz", 0, 8), rows("b5", 8, 16), rows(st, 0, 8), A.mult)
+            act(W("Kb"), rows("b3", 4, 12), F.Copy)
         def memory_sums():
-            for j, mzr in ((0, 4), (1, 0)):
+            for j, mzr in ((0, 0), (1, 4)):
                 ev, od = (4, 0) if t < 2 else (0, 4)
                 se, so = (do, de) if t < 2 else (0, 0)
                 for (a, b, c) in pieces(se):
                     r = rows("b0", 8 * j + ev + a, 8 * j + ev + b)
-                    mm(r, W("J1"), rows("kab", 8 * j + c, 8 * j + c + b - a), True, False)
-                    mm(r, W("J1"), rows("mz", mzr + c, mzr + c + b - a), False, True)
+                    mm(r, W("IH"), rows("kab", 8 * j + c, 8 * j + c + b - a), True, False)
+                    mm(r, W("I2k"), rows("Kb", c, c + b - a), False, False)
+                    mm(r, W("IH"), rows("mz", mzr + c, mzr + c + b - a), False, False)
+                    mm(r, W("I2k"), rows("Mf", c, c + b - a), False, True)
                 for (a, b, c) in pieces(so):
-                    mm(rows("b0", 8 * j + od + a, 8 * j + od + b), W("J1"), rows("kab", 8 * j + 4 + c, 8 * j + 4 + c + b - a), True, True)
-            if t < 2:
-                act(rows(out, 16, 32), W("b0"), F.Copy)
-                act(rows(out, 32, 33), rows("b3", 12, 13), F.Copy)
-                send(rank + 1, rows("st%d" % (t + 1), 16, 33), rows(out, 16, 33), "s%db" % (t + 1))
-            else:
-                for j in (0, 1):
-                    for h in (0, 1): act(X("foab", j, S(0, 4), h), rows("b0", 8 * j + 4 * h, 8 * j + 4 * h + 4), F.Identity, bias=4095.0, scale=-1.0)
-                send(rank - 2, W("fiab"), W("foab"), "fab")
+                    r = rows("b0", 8 * j + od + a, 8 * j + od + b)
+                    mm(r, W("IH"), rows("kab", 8 * j + 4 + c, 8 * j + 4 + c + b - a), True, False)
+                    mm(r, W("I2k"), rows("Kb", 4 + c, 4 + c + b - a), False, True)
+        def goals():
+            for j in range(16):
+                mm(X("b1", j), X("BH", j), W("code"), True, True)
+        ec = [NB * (M * (e - 1) - e * (e - 1) // 2) for e in range(M + 1)]
+        def pair(e):
+            if e == 0: tt(W("eq"), rows("b1", 0, 16), rows("own", 0, 16), A.is_equal)
+            else: tt(X("ee", S(0, 16), S(ec[e], ec[e + 1])), X("b1", S(0, 16), S(0, NB), S(0, M - e)), X("own", S(0, 16), S(0, NB), S(e, M)), A.is_equal)
+        out = "po%d" % (t + 1)
         if t < 2:
-            index_rest(out)
-            send(rank + 1, rows("st%d" % (t + 1), 0, 16), rows(out, 0, 16), "s%da" % (t + 1))
-        memories()
+            index_stage(out, "lo%d" % (t + 1), first_goals, goals, pair)
+            send(rank + 1, W("l%d" % (t + 1)), W("lo%d" % (t + 1)), "l%d" % (t + 1))
+            keeps()
+        else:
+            first_goals()
+            keeps()
+            places_e(); places_o()
+            goals()
+            places_b()
+            memories()
+            memory_sums()
+            for h in (0, 1): ts(rows("fog", 4 * h, 4 * h + 4), rows("b%d" % (6 + h), 0, 4), -1.0, 2048.0, A.mult, A.add)
+            send(rank - 2, W("fig"), W("fog"), "fg")
+        off = X("lgg", S(0, 64))
+        emit("s", lambda: s.activation(T.gab[:], T.win[:, 0:4096].indirect(off[0]), F.Copy), [X("win", S(0, 4096)), off], [W("gab")])
+        pe = X("b7" if t < 2 else "b5", S(8, 10), S(0, NE // 2))
+        def count(lo, hi):
+            for j in range(lo, min(hi, 15)): mm(X("b2", 0), X("MK", j), X("eq", j), False, False)
+            for j in range(lo, hi): mm(pe, W("I1"), X("ee", j), j == 0, j == 15)
+        mm(X("b2", 0), W("IH"), W("code"), True, False)
+        mm(W("b4"), W("cmh"), W("on5"), True, False)
+        for h in (0, 1): mm(W("b4"), W("I1"), X("gab", S(512 * h, 512 * h + 512)), False, h == 1)
+        act(W("vf"), W("b4"), F.Identity, bias=8388608.0, scale=0.5)
+        act(W("vals"), W("vf"), F.Identity, bias=-8388608.0)
+        for e in (0, 1, 2) if t < 2 else (0, 1, 2, 3): pair(e)
+        count(0, 16)
+        if t < 2:
+            send(rank + 1, rows("st%d" % (t + 1), 0, 8), rows(out, 0, 8), "s%da" % (t + 1))
+            memories()
+        else:
+            ts(W("foab"), W("b0"), -1.0, 4095.0, A.mult, A.add)
+            send(rank - 2, W("fiab"), W("foab"), "fab")
         cp(W("ce"), pe)
         for e in range(1, M): mm(X("b2", 0, S(0, NB), S(e, M)), W("I8k"), X("ce", S(ec[e], ec[e + 1])), False, e == M - 1)
-        memory_sums()
-        tt(W("dm"), X("b2", 0), X("fall", 0), A.min)
-        cp(W("dst"), W("dm"))
+        if t < 2:
+            index_rest(out)
+            memory_sums()
+            act(rows(out, 24, 32), rows("b0", 8, 16), F.Identity, bias=-2048.0)
+            act(rows(out, 32, 33), rows("b3", 12, 13), F.Copy)
+            send(rank + 1, rows("st%d" % (t + 1), 24, 33), rows(out, 24, 33), "s%db" % (t + 1))
+            act(rows(out, 16, 24), rows("b0", 0, 8), F.Identity, bias=-2048.0)
+            send(rank + 1, rows("st%d" % (t + 1), 8, 24), rows(out, 8, 24), "s%dc" % (t + 1))
+        for u in range(M):
+            ts(X("dst", S(u, 32, M)), X("b2", 0, S(0, NB), u), X("fall", S(u, u + 1)), 2048.0, A.min, A.add)
         for q in range(NB - 1, -1, -1):
             off2, va, wn = X("dst", S(q * M, q * M + M)), X("vals", S(16 * M * q, 16 * M * (q + 1))), W("win")
             emit("v", lambda: v.tensor_copy(T.win[:, 0:4608].indirect(off2[0]), va[0]), [off2, va], [wn])
@@ -420,7 +466,7 @@ def rank_program(g, core, T, topo):
     for t in range(3): visit(t)
     cp(X("win", S(4095, 4096)), X("sv", S(0, 1)))
     dma("y", T.ox[:], T.win[:, 0:4096], [X("win", S(0, 4096))], [])
-    dma("s", T.og[:], T.fig[:], [W("fig")], [])
-    dma("s", T.oa[:], T.fiab[:, 0], [X("fiab", 0)], [])
-    dma("y", T.ob[:], T.fiab[:, 1], [X("fiab", 1)], [])
+    for src, r0, buf, dst in (("fig", 0, "og_", T.og), ("fiab", 8, "oa_", T.oa), ("fiab", 0, "ob_", T.ob)):
+        for h in (0, 1): cp(X(buf, S(0, 4), h), rows(src, r0 + 4 * h, r0 + 4 * h + 4))
+        dma("y" if buf == "ob_" else "s", dst[:], T[buf][:], [W(buf)], [])
     for sem in cnt: g.wait_ge(T.sem[sem], cnt[sem])

import numpy as np
from concourse.mybir import AluOpType as A, ActivationFunctionType as F

M = 4
NB = 32 // M
NE = NB * M * (M - 1) // 2
f32, f16, bf, i32, u16 = "float32", "float16", "bfloat16", "int32", "uint16"
SCRATCH = {
    "win": ("sbuf", [128, 4608], bf), "sv": ("sbuf", [128, 16], bf),
    "yv0": ("sbuf", [128, 1024], bf), "yv1": ("sbuf", [128, 1024], bf), "yv2": ("sbuf", [128, 1024], bf),
    "yi1": ("sbuf", [128, 1024], bf), "yi2": ("sbuf", [128, 1024], bf),
    "gn": ("sbuf", [128, 4, 2, 32], i32), "an": ("sbuf", [128, 4, 2, 32], i32), "bn": ("sbuf", [128, 4, 2, 32], i32),
    "tn": ("sbuf", [128, 4, 2, 32], i32), "tf0": ("sbuf", [128, 8, 32], f32),
    "ti1": ("sbuf", [128, 8, 32], f32), "ti2": ("sbuf", [128, 8, 32], f32),
    "l0": ("sbuf", [128, 384], u16), "l1": ("sbuf", [128, 384], u16), "l2": ("sbuf", [128, 384], u16),
    "lo1": ("sbuf", [128, 384], u16), "lo2": ("sbuf", [128, 384], u16),
    "dd": ("sbuf", [128, 6144], bf), "ab": ("sbuf", [128, 6144], bf),
    "E": ("sbuf", [128, 8, 32], bf), "AE": ("sbuf", [128, 8, 32], bf), "O": ("sbuf", [128, 8, 32], bf),
    "UX": ("sbuf", [128, 8, 32], bf), "Mf": ("sbuf", [128, 4, 32], bf),
    "Eo": ("sbuf", [128, 4, 32], bf), "Cb": ("sbuf", [128, 1, 32], bf),
    "thr": ("sbuf", [128, 8, 32], f32), "dsb": ("sbuf", [128, 8, 32], f32), "mn": ("sbuf", [128, 4, 32], f32),
    "nv": ("sbuf", [128, 12, 32], f32), "keys": ("sbuf", [128, 12, 32], f16), "fall": ("sbuf", [128, 32], f32),
    "fallc": ("sbuf", [128, 32], f32), "code": ("sbuf", [128, 32], f16), "BH": ("sbuf", [128, 16, 128], f16), "IH": ("sbuf", [128, 128], f16),
    "Kb": ("sbuf", [128, 8, 32], bf),
    "xg": ("sbuf", [128, 512], bf), "zz": ("sbuf", [128, 16, 128], bf), "Tf": ("sbuf", [128, 8, 32], bf), "Ff": ("sbuf", [128, 4, 32], bf), "lgg": ("sbuf", [128, 64], u16), "hi": ("sbuf", [128, 32], bf),
    "lw": ("sbuf", [128, 32], bf), "own": ("sbuf", [128, 16, NB, M], f32), "eq": ("sbuf", [128, 16, 32], bf), "ee": ("sbuf", [128, 16, NE], bf), "ce": ("sbuf", [128, NE], bf),
    "gab": ("sbuf", [128, 1024], bf), "vf": ("sbuf", [128, 512], f32), "vals": ("sbuf", [128, 512], bf), "dm": ("sbuf", [128, 32], i32),
    "dst": ("sbuf", [128, 32], u16),
    "oab": ("sbuf", [128, 16, 32], f16), "kab": ("sbuf", [128, 16, 32], f16), "mz": ("sbuf", [128, 8, 32], f16),
    "vz": ("sbuf", [128, 12, 32], f16), "X": ("sbuf", [128, 8, 32], f32),
    "P": ("sbuf", [128, 8, 32], i32), "H": ("sbuf", [128, 8, 32], i32), "NQ": ("sbuf", [128, 8, 32], i32),
    "IDX": ("sbuf", [128, 8, 32], i32),
    "fog": ("sbuf", [128, 8, 32], u16), "foab": ("sbuf", [128, 16, 32], u16),
    "fig": ("sbuf", [128, 8, 32], u16), "fiab": ("sbuf", [128, 16, 32], u16),
    "og_": ("sbuf", [128, 4, 2, 32], f32), "oa_": ("sbuf", [128, 4, 2, 32], f32), "ob_": ("sbuf", [128, 4, 2, 32], f32),
    "ones": ("sbuf", [128, 256], bf), "on5": ("sbuf", [128, 512], bf), "SS": ("sbuf", [128, 2048], bf), "BB": ("sbuf", [128, 16, 128], bf),
    "MK": ("sbuf", [128, 16, 128], bf), "SG": ("sbuf", [128, 128], bf),
    "pi": ("sbuf", [128, 1], i32), "pa": ("sbuf", [128, 1], i32), "pb": ("sbuf", [128, 1], i32),
    "pm": ("sbuf", [128, 1], f32), "pg": ("sbuf", [128, 1], f32), "io8": ("sbuf", [128, 8], f32),
    "iop": ("sbuf", [128, 8, 16], f32), "bm8": ("sbuf", [128, 8], f32), "ioi": ("sbuf", [128, 32], f32),
}
for _n in ("st0", "st1", "st2", "po1", "po2"):
    SCRATCH[_n] = ("sbuf", [128, 33, 32], f32)
WB = {"I1": 1, "Im1": -1, "I8k": 8192, "Im8k": -8192, "I16k": 16384, "Im16k": -16384, "I1920": 1920, "I28": 28, "I2k": 2048, "Im2k": -2048}
WF = {"J1": 1, "Jm1": -1, "Jm101": -101, "Jm129": -129}
CM = {"c230": -230 / 128, "cm1": -1 / 128, "c2k": 16.0, "cp1": 1 / 128, "cmh": -0.5 / 128, "c8k": 64.0}
for _n in WB: SCRATCH[_n] = ("sbuf", [128, 128], bf)
for _n in WF: SCRATCH[_n] = ("sbuf", [128, 128], f32)
for _n in CM: SCRATCH[_n] = ("sbuf", [128, 128], bf)
for _n in ("b0", "b3", "b4", "b5", "b6", "b7"): SCRATCH[_n] = ("psum", [128, 16, 32], f32)
for _n in ("b1", "b2"): SCRATCH[_n] = ("psum", [128, 16, NB, M], f32)
NDMA = 16
HELP = True
ARR = ["yi1", "yi2", "ti1", "ti2", "l1", "l2", "s1a", "s1b", "s1c", "s2a", "s2b", "s2c", "fg", "fab"]
SEMAPHORES = ["qv", "qs", "qt", "qg", "loc"] + ["d%d" % k for k in range(NDMA)] + ["a_" + n for n in ARR]
_cache = {}


def rank_program(g, core, T, topo):
    rank = T.rank_of(core)
    if rank is None:
        return
    N = len(T.cores)
    eng = {"v": g.vector, "s": g.scalar, "t": g.tensor, "g": g, "y": g.sync}
    cnt = {}
    known = {q: {} for q in eng}
    hist = {n: [] for n in SCRATCH}

    def X(name, *idx):
        key = (name,) + tuple(("s", i.start, i.stop, i.step) if isinstance(i, slice) else i for i in idx)
        if key not in _cache:
            shp = SCRATCH[name][1][1:]
            a = np.arange(int(np.prod(shp))).reshape(shp)[idx].ravel()
            b = np.zeros(int(np.prod(shp)), np.uint8)
            b[a] = 1
            _cache[key] = int.from_bytes(np.packbits(b).tobytes(), "big")
        return (T[name][(slice(None),) + idx], name, _cache[key])

    def sync(q, rd, wr):
        need = {}
        for regs, w in ((rd, False), (wr, True)):
            for r in regs:
                psum = SCRATCH[r[1]][0] == "psum"
                for (m, pw, pq, sem, c, clk) in hist[r[1]]:
                    if psum and pq != q:
                        hit = True
                    elif psum and q == "t":
                        hit = False
                    else:
                        hit = bool(m & r[2]) and (pw or w)
                    if hit and known[q].get(sem, 0) < c and (sem not in need or need[sem][0] < c):
                        need[sem] = (c, clk)
        for sem in sorted(need, key=lambda s: -len(need[s][1])):
            c, clk = need[sem]
            if known[q].get(sem, 0) >= c: continue
            eng[q].wait_ge(T.sem[sem], c)
            for k in clk: known[q][k] = max(known[q].get(k, 0), clk[k])

    def record(q, rd, wr, sem, c):
        clk = dict(known[q]); clk[sem] = c
        for regs, w in ((rd, False), (wr, True)):
            for r in regs:
                h = hist[r[1]]
                if w:
                    h[:] = [e for e in h if (e[0] & ~r[2]) or clk.get(e[3], 0) < e[4]]
                else:
                    h[:] = [e for e in h if e[1] or e[2] != q or (e[0] & ~r[2])]
                h.append((r[2], w, q, sem, c, clk))

    def emit(q, call, rd, wr):
        sem = "q" + q
        sync(q, rd, wr)
        cnt[sem] = cnt.get(sem, 0) + 1
        call().then_inc(T.sem[sem], 1)
        record(q, rd, wr, sem, cnt[sem])

    v, s, te = g.vector, g.scalar, g.tensor
    def tt(o, a, b, op): emit("v", lambda: v.tensor_tensor(o[0], a[0], b[0], op), [a, b], [o])
    def ts(o, a, s1, s2, op0, op1=None):
        sc = [x for x in (s1,) if isinstance(x, tuple)]
        p1 = s1[0] if sc else s1
        if op1 is None: emit("v", lambda: v.tensor_scalar(o[0], a[0], p1, None, op0), [a] + sc, [o])
        else: emit("v", lambda: v.tensor_scalar(o[0], a[0], p1, s2, op0, op1), [a] + sc, [o])
    def cp(o, a): emit("v", lambda: v.tensor_copy(o[0], a[0]), [a], [o])
    def ms(o, c): emit("v", lambda: v.memset(o[0], c), [], [o])
    def act(o, a, f=F.Identity, bias=0.0, scale=1.0):
        if isinstance(scale, tuple): emit("s", lambda: s.activation(o[0], a[0], f, scale=scale[0]), [a, scale], [o])
        elif bias == 0.0: emit("s", lambda: s.activation(o[0], a[0], f, scale=scale), [a], [o])
        else: emit("s", lambda: s.activation(o[0], a[0], f, bias=bias, scale=scale), [a], [o])
    def mm(o, w, r, first, last): emit("t", lambda: te.matmul(o[0], w[0], r[0], first, last), [w, r], [o])
    W = lambda n: X(n)
    ndma = [0]
    def dma(q, o, a, rd, wr):
        sem = "d%d" % ndma[0]; ndma[0] += 1
        sync(q, rd, wr)
        eng[q].dma_start(o, a).then_inc(T.sem[sem], 16)
        cnt[sem] = 16
        record(q, rd, wr, sem, 16)
    def nengines(a, b): return len(topo.engines(a, b))
    def send(to, o, i, sem):
        dst = T.cores[to % N]
        sync("g", [i], [])
        rid, pid, _ = topo.addr(dst)
        cnt["loc"] = cnt.get("loc", 0) + nengines(core, dst)
        g.remote_dma(o[0], i[0], T.sem["a_" + sem], T.sem.loc, pid, rid, topo.mask(core, dst))
    def arrives(frm, sem, o):
        c = nengines(T.cores[frm % N], core)
        cnt["a_" + sem] = c
        hist[o[1]].append((o[2], True, "r", "a_" + sem, c, {"a_" + sem: c}))
    S = slice
    def rows(n, a, b): return X(n, S(a, b))

    dma("y", T.gn[:], T.gl[:], [], [W("gn")])
    dma("y", T.win[:, 0:4096], T.xt[:], [], [X("win", S(0, 4096))])
    for k in (0, 1, 2):
        if k == 1:
            for n, src in (("an", T.al), ("bn", T.bl), ("tn", T.th)): dma("y", T[n][:], src[:], [], [W(n)])
        for h in (0, 1)[:2 if k == 0 else 1]:
            n = "yv%d" % k
            dma("y", T[n][:, h * 512:h * 512 + 512], T.yv[:, k * 512:k * 512 + 512], [], [X(n, S(h * 512, h * 512 + 512))])
    for k in (1, 2):
        arrives(rank - k, "yi%d" % k, X("yi%d" % k, S(0, 512)))
        arrives(rank - k, "ti%d" % k, W("ti%d" % k))
        n = T["yi%d" % k]
        dma("y", n[:, 512:1024], n[:, 0:512], [X("yi%d" % k, S(0, 512))], [X("yi%d" % k, S(512, 1024))])
    for k in (1, 2):
        arrives(rank - 1, "l%d" % k, W("l%d" % k))
        arrives(rank - 1, "s%da" % k, rows("st%d" % k, 0, 8))
        arrives(rank - 1, "s%db" % k, rows("st%d" % k, 24, 33))
        arrives(rank - 1, "s%dc" % k, rows("st%d" % k, 8, 24))
    arrives(rank + 2, "fg", W("fig")); arrives(rank + 2, "fab", W("fiab"))

    emit("g", lambda: g.iota(T.pi[:], [[0, 1]], 0, 1), [], [W("pi")])
    ms(W("ones"), 1.0)
    big = dict(allow_small_or_imprecise_dtypes=True)
    emit("g", lambda: g.affine_select(T.I1[:], T.ones[:, 0:128], [[-1, 128]], A.is_equal, 0.0, 0, 1), [X("ones", S(0, 128))], [W("I1")])
    emit("g", lambda: g.iota(T.io8[:], [[1, 8]], 0, 0, **big), [], [W("io8")])
    emit("g", lambda: g.iota(T.iop[:], [[0, 8], [1, 16]], 0, 0, **big), [], [W("iop")])
    emit("g", lambda: g.iota(T.ioi[:], [[16, 32]], 2048, 0, **big), [], [W("ioi")])
    ms(W("zz"), 0.0)
    emit("g", lambda: g.affine_select(T.BB[:], T.zz[:], [[-1, 16], [-16, 8], [0, 16]], A.not_equal, 1.0, 0, 1), [W("zz")], [W("BB")])
    for n in CM: ms(W(n), CM[n])
    ts(W("pa"), W("pi"), 15, None, A.bitwise_and)
    ts(W("pb"), W("pi"), 4, None, A.arith_shift_right)
    cp(W("pm"), W("pa")); cp(W("pg"), W("pb"))
    ts(W("bm8"), W("io8"), W("pg"), None, A.is_equal)
    ts(W("SG"), W("iop"), W("pm"), None, A.is_equal)
    ts(W("fall"), W("ioi"), W("pm"), None, A.add)
    ts(W("fallc"), W("fall"), 2.0, -2046.0, A.mult, A.add)
    cp(W("IH"), W("I1"))
    for n in ("J1", "Jm1", "Jm101", "Jm129"): act(W(n), W("I1"), F.Identity, scale=float(WF[n]))
    for n in ("I1920", "I28"): act(W(n), W("I1"), F.Identity, scale=float(WB[n]))

    def pieces(sh): return {0: [(0, 4, 0)], 1: [(0, 3, 1), (3, 4, 0)], -1: [(1, 4, 0), (0, 1, 3)]}[sh]
    def add(bank, base, w, src, sbase, sh, first=False, last=False):
        ps = pieces(sh)
        for j, (a, b, c) in enumerate(ps):
            mm(rows(bank, base + a, base + b), W(w), rows(src, sbase + c, sbase + c + b - a), first and j == 0, last and j == len(ps) - 1)

    def index_stage(po, lo, meanwhile=None, goals=None, pair=None):
        ts(rows("X", 4, 8), rows("b7", 0, 4), -2047.0, -4127.0, A.is_equal, A.mult)
        act(rows(po, 0, 4), rows("b7", 0, 4), F.Identity, bias=-1.0)
        act(W("Eo"), rows("b7", 0, 4), F.Relu, bias=-2046.0, scale=-1.0)
        ts(X(lo, S(0, 128)), rows("b6", 0, 4), -1.0, 2048.0, A.mult, A.add)
        tt(rows("P", 4, 7), rows("X", 4, 7), rows("b6", 1, 4), A.mult)
        tt(rows("P", 7, 8), rows("X", 7, 8), rows("b6", 0, 1), A.mult)
        act(rows("X", 0, 4), rows("b6", 0, 4), F.Identity, bias=2048.0)
        act(rows(po, 4, 8), rows("b6", 0, 4), F.Identity, bias=-1.0)
        if meanwhile: meanwhile()
        tt(rows("P", 0, 4), rows("X", 0, 4), rows("b7", 0, 4), A.mult)
        one = X("ones", S(0, 128))
        mm(rows("b5", 4, 8), W("cm1"), one, True, False)
        mm(rows("b5", 4, 8), W("c2k"), one, False, False)
        add("b5", 4, "Jm1", po, 0, 0)
        add("b5", 4, "I1920", "Eo", 0, 0)
        add("b5", 4, "I28", "Eo", 0, 0, last=True)
        mm(rows("b5", 0, 4), W("c230"), one, True, False)
        add("b5", 0, "Jm129", po, 0, 0)
        add("b5", 0, "Jm101", po, 4, 0, last=True)
        ts(W("H"), W("P"), 5, None, A.arith_shift_right)
        if goals: goals()
        tt(W("NQ"), W("H"), rows("b5", 0, 8), A.add)
        ts(W("IDX"), W("NQ"), 4095, None, A.bitwise_and)
        if pair: pair(3)
        cp(X(lo, S(128, 384)), W("IDX"))

    def index_rest(po):
        ts(rows(po, 8, 16), W("IDX"), -1.0, 2047.0, A.mult, A.add)

    for h in (0, 1): ts(rows("b%d" % (6 + h), 0, 4), X("gn", S(0, 4), h), -1.0, 2048.0, A.mult, A.add)
    index_stage("st0", "l0")
    act(W("SS"), W("zz"), F.Copy)
    for e in range(8):
        act(X("SS", S(16 * e, 16 * e + 129 * 15 + 1, 129)), X("ones", S(0, 16)), F.Identity, scale=X("bm8", S(e, e + 1)))
    for n in ("Im1", "I8k", "Im8k", "I16k", "Im16k", "I2k", "Im2k"): act(W(n), W("I1"), F.Identity, scale=float(WB[n]))
    def home_rest():
        index_rest("st0")
        for n, b in (("an", 24), ("bn", 16)):
            for h in (0, 1): ts(rows("st0", b + 4 * h, b + 4 * h + 4), X(n, S(0, 4), h), -1.0, 2047.0, A.mult, A.add)
        for h in (0, 1): cp(rows("tf0", 4 * h, 4 * h + 4), X("tn", S(0, 4), h))
        for k in (1, 2): send(rank + k, W("ti%d" % k), W("tf0"), "ti%d" % k)
    for k in (1, 2): send(rank + k, X("yi%d" % k, S(0, 512)), X("yv%d" % k, S(0, 512)), "yi%d" % k)
    def goal_constants():
        act(W("on5"), X("zz", S(0, 4)), F.Identity, bias=1.0)
        emit("g", lambda: g.affine_select(T.MK[:], T.zz[:], [[0, 16], [-16, 8], [-1, 16]], A.not_equal, 8192.0, 0, 1), [W("zz")], [W("MK")])
        emit("g", lambda: g.affine_select(T.MK[:], T.MK[:], [[-1, 16], [0, 8], [1, 16]], A.is_gt, 0.0, 0, 0), [W("MK")], [W("MK")])
    cp(W("BH"), W("BB"))
    cp(X("sv", S(0, 1)), X("win", S(4095, 4096)))
    ms(X("win", S(4095, 4096)), 512.0)

    CALLS = [(0, 64), (64, 64), (256, 64), (320, 64), (128, 64), (192, 32 if HELP else 64)]
    def visit(t):
        st, ls, yv, th = "st%d" % t, "l%d" % t, ("yi%d" % t if t else "yv0"), ("ti%d" % t if t else "tf0")

        def gather(c, n):
            e = 16 * n
            o, off, vw, wn = X("dd", S(16 * c, 16 * c + e)), X(ls, S(c, c + n)), X(yv, S(0, e)), X("win", S(0, 4096))
            emit("v", lambda: v.tensor_tensor(o[0], T.win[:, 0:4096].indirect(off[0]), vw[0], A.subtract), [wn, off, vw], [o])
        def size(c, n): act(X("ab", S(16 * c, 16 * c + 16 * n)), X("dd", S(16 * c, 16 * c + 16 * n)), F.Abs)
        def total(c, n):
            bank, r0 = ("b1", (c - 128) // 32) if 128 <= c < 256 else ("b0", c // 32 if c < 128 else c // 32 - 4)
            for j in range(16):
                mm(rows(bank, r0, r0 + n // 32), X("SS", S(128 * j, 128 * j + 128)), X("ab", S(16 * c + j, 16 * c + 16 * n, 16)),
                   j == 0 and bank == "b0", j == 15 and (bank == "b0" or c == 192))
        def prep_a():
            act(rows("E", 0, 4), rows(st, 4, 8), F.Relu, bias=-2047.0, scale=-1.0)
            act(rows("E", 4, 8), rows(st, 0, 4), F.Relu, bias=-2047.0, scale=-1.0)
            mm(rows("b6", 0, 8), W("I16k"), rows("E", 0, 8), True, False)
            add("b6", 0, "Im16k", "E", 4, 0)
            add("b6", 4, "Im16k", "E", 0, 1)
            if t == 1:
                add("b6", 0, "J1", th, 4, 0); add("b6", 4, "J1", th, 0, 1)
            else:
                mm(rows("b6", 0, 8), W("J1"), rows(th, 0, 8), False, False)
        def prep_b():
            act(W("AE"), rows(st, 24, 32), F.Relu, bias=-2047.0, scale=-1.0)
            if t: act(W("Cb"), rows(st, 32, 33), F.Copy)
            mm(rows("b6", 0, 8), W("I16k"), rows("AE", 0, 8), False, t == 0)
            if t:
                for k in range(8): mm(rows("b6", k, k + 1), W("I1"), W("Cb"), False, k == 7)

        one, o1 = X("ones", S(0, 256)), X("ones", S(0, 128))
        def empty_gates():
            mm(rows("b3", 0, 4), W("Im1"), rows("E", 0, 4), True, False)
            mm(rows("b2", 0, 8), W("I1"), W("E"), True, False)
            add("b2", 4, "Im1", "E", 0, 1)
            mm(rows("b4", 0, 12), W("I1"), X("zz", S(0, 3)), True, False)
            mm(rows("b4", 0, 4), W("I1"), o1, False, False)
            mm(rows("b4", 8, 12), W("I1"), o1, False, False)
            add("b4", 8, "Im1", "E", 4, 0)
        def open_gates():
            add("b3", 0, "Im1", "O", 4, 0)
            add("b2", 0, "Im1", "O", 4, -1)
            add("b2", 4, "Im1", "O", 0, 0)
            add("b4", 0, "Im1", "O", 0, 0)
            add("b4", 8, "Im1", "O", 4, 0)
        de, do = (0, 1) if t == 0 else (-1, 0) if t == 1 else (0, 0)
        be, bo = ("b7", "b6") if t < 2 else ("b6", "b7")
        def places_0():
            for bank in (be, bo):
                mm(rows(bank, 0, 4), W("cp1"), o1, True, False)
        def places_e():
            add(be, 0, "IH", "oab", 8, do)
            add(be, 0, "IH", "oab", 4, do - 1)
            add(be, 0, "I2k", "O", 4, do - 1)
        def places_o():
            add(bo, 0, "IH", "oab", 12, de)
            add(bo, 0, "IH", "oab", 0, de)
            add(bo, 0, "I2k", "O", 0, de)
            add(bo, 0, "Im2k", "E", 4, de)
        if HELP:
            off0 = X(ls, S(224, 256))
            emit("s", lambda: s.activation(T.xg[:], T.win[:, 0:4096].indirect(off0[0]), F.Copy), [X("win", S(0, 4096)), off0], [W("xg")])
        for k, (c, n) in enumerate(CALLS):
            gather(c, n)
            if k == 1 and t == 0:
                home_rest()
                goal_constants()
            if k == 4:
                tt(W("O"), rows("b0", 0, 8), W("thr"), A.is_gt)
                mm(rows("b5", 0, 8), W("I1"), W("O"), True, True)
                mm(rows("b5", 8, 16), W("I1"), W("O"), True, True)
            if k == len(CALLS) - 1: tt(W("oab"), W("b5"), rows(st, 16, 32), A.mult)
            if k == 3: prep_b()
            size(c, n)
            if k == 2: prep_a()
            if k == 4:
                act(W("dsb"), rows("b0", 0, 8), F.Copy)
                mm(rows("b1", 0, 4), W("I8k"), rows("E", 4, 8), True, False)
            if k == 0 and HELP:
                mm(W("b4"), W("I1"), W("xg"), True, False)
                mm(W("b4"), W("Im1"), X(yv, S(0, 512)), False, True)
            if k == 1 and HELP: act(X("ab", S(16 * 224, 16 * 256)), W("b4"), F.Abs)
            if k < 5: total(c, n)
            if k == 3:
                act(W("thr"), rows("b6", 0, 8), F.Identity, bias=16384.0)
                empty_gates()
            if k == 4: open_gates()
        act(W("nv"), rows(st, 0, 12), F.Identity, bias=-1.0, scale=-1.0)
        total(192, 64)
        places_0()
        tt(W("mn"), rows("b0", 0, 4), rows("dsb", 4, 8), A.min)
        tt(rows("UX", 4, 7), rows("b0", 4, 7), rows("dsb", 1, 4), A.is_lt)
        tt(rows("UX", 7, 8), rows("b0", 7, 8), rows("dsb", 0, 1), A.is_lt)
        add("b2", 4, "I1", "UX", 4, 0)
        tt(rows("UX", 0, 4), rows("b1", 0, 4), W("mn"), A.is_lt)
        add("b3", 0, "I1", "UX", 0, 0, last=True)
        add("b2", 0, "I1", "UX", 0, 0, last=True)
        ts(W("Mf"), rows("b3", 0, 4), 0.0, None, A.max)
        act(W("Tf"), rows("b2", 0, 8), F.Relu, bias=-1.0)
        if t < 2: places_e()
        mm(rows("b3", 4, 8), W("I1"), W("Mf"), True, False)
        for k in (1, 2, 3): mm(rows("b3", 4 + k, 8), W("Im1"), rows("Mf", 0, 4 - k), False, k == 3)
        act(W("Ff"), rows("b3", 4, 8), F.Relu)
        add("b4", 0, "Im1", "Mf", 0, 0)
        add("b4", 4, "I1", "Mf", 0, 0)
        add("b4", 8, "Im1", "Mf", 0, 0)
        mm(rows("b4", 4, 12), W("I1"), W("Tf"), False, True)
        if t < 2: places_o()
        for k in range(3): mm(rows("b2", 4 * k, 4 * k + 4), W("I1"), W("Ff"), True, True)
        for k in range(2): mm(rows("b5", 8 + 4 * k, 12 + 4 * k), W("I1"), W("Mf"), True, True)
        tt(W("vz"), rows("b4", 0, 12), rows(st, 4, 16), A.mult)
        tt(W("keys"), rows("b2", 0, 12), W("nv"), A.mult)
        def places_b():
            add(be, 0, "I2k", "Tf", 0, do)
            add(bo, 0, "I2k", "Tf", 4, de)
            add(bo, 0, "Im2k", "Mf", 0, de)
            add(be, 0, "IH", "vz", 0, do)
            add(be, 0, "IH", "vz", 4, do, last=True)
            add(bo, 0, "IH", "vz", 8, de, last=True)
        if t < 2: places_b()
        for a in range(4): mm(rows("b3", 8, 11), W("IH"), X("keys", S(a, 12, 4)), a == 0, False)
        mm(rows("b3", 10, 11), W("c8k"), X("ones", S(0, 32)), False, False)
        for a in range(4): mm(rows("b3", 10, 11), W("Im8k"), rows("Ff", a, a + 1), False, a == 3)
        def first_goals():
            tt(W("code"), rows("b3", 10, 11), W("fallc"), A.min)
            for k in range(4): tt(X("own", k), rows("b3", 10, 11), W("fallc"), A.min)
            ts(W("lgg"), rows("b3", 8, 10), 2048.0, None, A.add)
            for k in (4, 8): act(rows("own", k, 2 * k), rows("own", 0, k), F.Copy)
        def keeps():
            mm(rows("b3", 4, 12), W("I1"), one, True, False)
            mm(rows("b3", 4, 12), W("Im1"), W("O"), False, False)
            mm(rows("b3", 4, 12), W("Im1"), W("Tf"), False, False)
            add("b3", 4, "Im1", "Mf", 0, 0)
            add("b3", 4, "Im1", "O", 4, -1)
            add("b3", 8, "Im1", "O", 0, 0)
            add("b3", 8, "Im1", "Mf", 0, 0, last=True)
            if t < 2:
                for a in range(4): mm(rows("b3", 12, 13), W("SG"), rows("Mf", a, a + 1), a == 0, a == 3)
        def memories():
            tt(rows("kab", 0, 8), rows("b3", 4, 12), rows(st, 16, 24), A.mult)
            tt(rows("kab", 8, 16), rows("b3", 4, 12), rows(st, 24, 32), A.mult)
            tt(rows("mz", 0, 8), rows("b5", 8, 16), rows(st, 0, 8), A.mult)
            act(W("Kb"), rows("b3", 4, 12), F.Copy)
        def memory_sums():
            for j, mzr in ((0, 0), (1, 4)):
                ev, od = (4, 0) if t < 2 else (0, 4)
                se, so = (do, de) if t < 2 else (0, 0)
                for (a, b, c) in pieces(se):
                    r = rows("b0", 8 * j + ev + a, 8 * j + ev + b)
                    mm(r, W("IH"), rows("kab", 8 * j + c, 8 * j + c + b - a), True, False)
                    mm(r, W("I2k"), rows("Kb", c, c + b - a), False, False)
                    mm(r, W("IH"), rows("mz", mzr + c, mzr + c + b - a), False, False)
                    mm(r, W("I2k"), rows("Mf", c, c + b - a), False, True)
                for (a, b, c) in pieces(so):
                    r = rows("b0", 8 * j + od + a, 8 * j + od + b)
                    mm(r, W("IH"), rows("kab", 8 * j + 4 + c, 8 * j + 4 + c + b - a), True, False)
                    mm(r, W("I2k"), rows("Kb", 4 + c, 4 + c + b - a), False, True)
        def goals():
            for j in range(16):
                mm(X("b1", j), X("BH", j), W("code"), True, True)
        ec = [NB * (M * (e - 1) - e * (e - 1) // 2) for e in range(M + 1)]
        def pair(e):
            if e == 0: tt(W("eq"), rows("b1", 0, 16), rows("own", 0, 16), A.is_equal)
            else: tt(X("ee", S(0, 16), S(ec[e], ec[e + 1])), X("b1", S(0, 16), S(0, NB), S(0, M - e)), X("own", S(0, 16), S(0, NB), S(e, M)), A.is_equal)
        out = "po%d" % (t + 1)
        if t < 2:
            index_stage(out, "lo%d" % (t + 1), first_goals, goals, pair)
            send(rank + 1, W("l%d" % (t + 1)), W("lo%d" % (t + 1)), "l%d" % (t + 1))
            keeps()
        else:
            first_goals()
            keeps()
            places_e(); places_o()
            goals()
            places_b()
            memories()
            memory_sums()
            for h in (0, 1): ts(rows("fog", 4 * h, 4 * h + 4), rows("b%d" % (6 + h), 0, 4), -1.0, 2048.0, A.mult, A.add)
            send(rank - 2, W("fig"), W("fog"), "fg")
        off = X("lgg", S(0, 64))
        emit("s", lambda: s.activation(T.gab[:], T.win[:, 0:4096].indirect(off[0]), F.Copy), [X("win", S(0, 4096)), off], [W("gab")])
        pe = X("b7" if t < 2 else "b5", S(8, 10), S(0, NE // 2))
        def count(lo, hi):
            for j in range(lo, min(hi, 15)): mm(X("b2", 0), X("MK", j), X("eq", j), False, False)
            for j in range(lo, hi): mm(pe, W("I1"), X("ee", j), j == 0, j == 15)
        mm(X("b2", 0), W("IH"), W("code"), True, False)
        mm(W("b4"), W("cmh"), W("on5"), True, False)
        for h in (0, 1): mm(W("b4"), W("I1"), X("gab", S(512 * h, 512 * h + 512)), False, h == 1)
        act(W("vf"), W("b4"), F.Identity, bias=8388608.0, scale=0.5)
        act(W("vals"), W("vf"), F.Identity, bias=-8388608.0)
        for e in (0, 1, 2) if t < 2 else (0, 1, 2, 3): pair(e)
        count(0, 16)
        if t < 2:
            send(rank + 1, rows("st%d" % (t + 1), 0, 8), rows(out, 0, 8), "s%da" % (t + 1))
            memories()
        else:
            ts(W("foab"), W("b0"), -1.0, 4095.0, A.mult, A.add)
            send(rank - 2, W("fiab"), W("foab"), "fab")
        cp(W("ce"), pe)
        for e in range(1, M): mm(X("b2", 0, S(0, NB), S(e, M)), W("I8k"), X("ce", S(ec[e], ec[e + 1])), False, e == M - 1)
        if t < 2:
            index_rest(out)
            memory_sums()
            act(rows(out, 24, 32), rows("b0", 8, 16), F.Identity, bias=-2048.0)
            act(rows(out, 32, 33), rows("b3", 12, 13), F.Copy)
            send(rank + 1, rows("st%d" % (t + 1), 24, 33), rows(out, 24, 33), "s%db" % (t + 1))
            act(rows(out, 16, 24), rows("b0", 0, 8), F.Identity, bias=-2048.0)
            send(rank + 1, rows("st%d" % (t + 1), 8, 24), rows(out, 8, 24), "s%dc" % (t + 1))
        for u in range(M):
            ts(X("dst", S(u, 32, M)), X("b2", 0, S(0, NB), u), X("fall", S(u, u + 1)), 2048.0, A.min, A.add)
        for q in range(NB - 1, -1, -1):
            off2, va, wn = X("dst", S(q * M, q * M + M)), X("vals", S(16 * M * q, 16 * M * (q + 1))), W("win")
            emit("v", lambda: v.tensor_copy(T.win[:, 0:4608].indirect(off2[0]), va[0]), [off2, va], [wn])

    for t in range(3): visit(t)
    cp(X("win", S(4095, 4096)), X("sv", S(0, 1)))
    dma("y", T.ox[:], T.win[:, 0:4096], [X("win", S(0, 4096))], [])
    for src, r0, buf, dst in (("fig", 0, "og_", T.og), ("fiab", 8, "oa_", T.oa), ("fiab", 0, "ob_", T.ob)):
        for h in (0, 1): cp(X(buf, S(0, 4), h), rows(src, r0 + 4 * h, r0 + 4 * h + 4))
        dma("y" if buf == "ob_" else "s", dst[:], T[buf][:], [W(buf)], [])
    for sem in cnt: g.wait_ge(T.sem[sem], cnt[sem])
